import numpy as np
import ml_dtypes


def mxq(x, axis, fmt="e4m3"):
    dtype, down = {"e4m3": (ml_dtypes.float8_e4m3fn, 7), "e5m2": (ml_dtypes.float8_e5m2, 14)}[fmt]
    v = np.moveaxis(np.asarray(x, np.float32).astype(ml_dtypes.bfloat16).astype(np.float64), axis, -1)
    blocks = v.reshape(v.shape[:-1] + (-1, 32))
    amax = np.abs(blocks).max(-1, keepdims=True)
    byte = np.maximum(np.where(amax > 0, np.frexp(amax)[1] - 1 + 127, 0) - down, 1)
    scale = np.exp2(byte - 127.0)
    codes = (blocks / scale).astype(np.float32).astype(dtype).astype(np.float64)
    return np.moveaxis((codes * scale).reshape(v.shape), -1, axis)


WIDE = False


def mx_kscale(k):
    if not WIDE:
        return np.ones(k)
    levels = np.array([24, -24, 12, -12, 0])
    if k % 512:
        return np.exp2(np.random.permutation(np.resize(levels, k // 32))).repeat(32)
    a = np.empty((k // 512, 16))
    for p in range(k // 512):
        a[p, :8] = np.random.permutation(np.resize(levels, 8))
        for g in range(8):
            far = levels[np.abs(levels - a[p, g]) >= 10]
            a[p, g + 8] = far[np.random.randint(len(far))]
    return np.exp2(a.ravel()).repeat(32)


def f64(x):
    return np.asarray(x).astype(np.float64)


def striped8(idx):
    return np.concatenate([v.reshape(-1, 16).T for v in idx]).astype(np.uint16)


def unstriped8(offs):
    return np.stack([offs[16 * g:16 * g + 16].T.reshape(-1) for g in range(8)]).astype(np.int64)


E2M1 = np.array([0.0, 0.5, 1.0, 1.5, 2.0, 3.0, 4.0, 6.0, -0.0, -0.5, -1.0, -1.5, -2.0, -3.0, -4.0, -6.0])


def pack_weight(w, fmt):
    k, n = w.shape
    w = f64(np.asarray(w, np.float32).astype(ml_dtypes.bfloat16)).reshape(k // 32, 32, n)
    amax = np.abs(w).max(1)
    if fmt == "e4m3":
        byte = np.frexp(amax)[1] - 1 + 127 - 7
    else:
        mant, ex = np.frexp(amax / 6.0)
        byte = np.where(mant > 0.5, ex, ex - 1) + 127
    byte = np.clip(np.where(amax > 0, byte, 1), 1, 254)
    scaled = (w * np.exp2(127.0 - byte)[:, None, :]).reshape(k, n).astype(np.float32)
    by_word = np.ascontiguousarray(scaled.reshape(k // 512, 128, 4, n).transpose(0, 1, 3, 2))
    if fmt == "e4m3":
        words = by_word.astype(ml_dtypes.float8_e4m3fn).view(np.uint8)
    else:
        c = by_word.astype(ml_dtypes.float4_e2m1fn).view(np.uint8) & 0xF
        words = (c[..., 0::2] | (c[..., 1::2] << 4)).reshape(k // 512, 128, 2 * n)
    return np.ascontiguousarray(words), np.ascontiguousarray(byte.astype(np.uint8).reshape(k // 512, 16, n))


def unpack_weight(words, scales, fmt):
    g, _, n = scales.shape
    words = np.ascontiguousarray(words).reshape(g, 128, n, -1)
    if fmt == "e4m3":
        vals = words.view(ml_dtypes.float8_e4m3fn).astype(np.float64)
    else:
        nib = np.empty((g, 128, n, 4), np.uint8)
        nib[..., 0::2] = words & 0xF
        nib[..., 1::2] = words >> 4
        vals = E2M1[nib]
    vals = vals * np.repeat(np.exp2(scales.astype(np.float64) - 127.0), 8, axis=1)[..., None]
    return vals.transpose(0, 1, 3, 2).reshape(g * 512, n)


def planes(y):
    n, m = y.shape
    v = y.astype(np.float32).astype(ml_dtypes.bfloat16).astype(np.float64).reshape(n // 32, 32, m)
    top = np.abs(v).max(1)
    byte = np.clip(np.where(top > 0, np.frexp(top)[1] - 1 + 127 - 7, 1), 1, 254)
    codes = (v * np.exp2(127.0 - byte)[:, None, :]).reshape(n, m).astype(np.float32).astype(ml_dtypes.float8_e4m3fn).view(np.uint8)
    words = codes.reshape(n // 512, 128, 4, m).transpose(0, 1, 3, 2)
    return np.ascontiguousarray(words), np.ascontiguousarray(byte.astype(np.uint8).reshape(n // 512, 16, m))


def gelu(f):
    return 0.5 * f * (1.0 + np.tanh(np.sqrt(2.0 / np.pi) * (f + 0.044715 * f**3)))


K, N, T, J = 512, 512, 2048, 512


def setup_inputs():
    n = np.random.standard_normal
    s = mx_kscale(K)[:, None]
    p_w = pack_weight(n((K, N)) / np.sqrt(K) / s, "e2m1")
    return {
        "xT": (n((K, T)) * s).astype(np.float32),
        "wgt": np.repeat(np.random.uniform(0.5, 2.0, (8, 3 * J)), 16, axis=0).astype(np.float32),
        "w_words": p_w[0],
        "w_scales": p_w[1],
        "b": (0.3 * n(N)).astype(np.float32),
        "offs": striped8(np.stack([np.concatenate([np.random.permutation(T)[:J] for _ in range(3)]) for _ in range(8)])),
    }


def reference(xT, wgt, w_words, w_scales, b, offs):
    idx = unstriped8(offs)
    rows = np.arange(K)
    xg = f64(wgt)[rows // 4 % 128] * f64(xT)[rows[:, None], idx[rows % 512 // 64]]
    xT_ = mxq(xg, 0, "e4m3").reshape(K, 3, J)
    w_ = unpack_weight(w_words, w_scales, "e2m1")
    a0 = w_.T @ xT_[:, 0]
    a1 = w_.T @ xT_[:, 1]
    a2 = w_.T @ xT_[:, 2]
    out_0 = gelu(np.maximum(np.maximum(a0, a1), a2) + f64(b)[:, None])
    return (out_0,) + planes(out_0)

@@ -1,0 +1,165 @@
+from contextlib import ExitStack
+
+import concourse.mybir as mybir
+
+K, N, T, J = 512, 512, 2048, 512
+PICKS = 3
+FLOPS = 2 * K * N * J * PICKS
+
+F32 = mybir.dt.float32
+BF16 = mybir.dt.bfloat16
+I32 = mybir.dt.int32
+U32 = mybir.dt.uint32
+U16 = mybir.dt.uint16
+U8 = mybir.dt.uint8
+FP8X4 = mybir.dt.float8_e4m3fn_x4
+FP4X4 = mybir.dt.float4_e2m1fn_x4
+MULT = mybir.AluOpType.mult
+MAX = mybir.AluOpType.max
+GELU = mybir.ActivationFunctionType.Gelu_apprx_tanh
+
+P = 128
+PACK = 4
+BANK = 512
+LIST_ROWS = 16
+CHUNKS = ((0, 256), (256, 256))
+
+
+def tile_list_max_geluP_kernel(tc, xT, wgt, w_words, w_scales, b, offs, out_0, out_1, out_2):
+    nc = tc.nc
+    with ExitStack() as ctx:
+        keep = ctx.enter_context(tc.tile_pool(name="keep", bufs=1))
+        ring = ctx.enter_context(tc.tile_pool(name="ring", bufs=3))
+        psum = ctx.enter_context(tc.psum_pool(name="psum", bufs=8))
+
+        offsets = keep.tile([P, PICKS * J // LIST_ROWS], U16, name="offsets")
+        planes = [keep.tile([P, T], F32, name="plane%d" % i) for i in range(PACK)]
+        weights = keep.tile([P, PICKS * J], F32, name="weights")
+        raw_words = keep.tile([P, 2 * N], U8, name="raw_words")
+        raw_scales = keep.tile([P, N], U8, name="raw_scales")
+        bias = keep.tile([P, PACK], F32, name="bias")
+        warm = keep.tile([P, 8], F32, name="warm")
+        warm2 = keep.tile([P, 8], F32, name="warm2")
+
+        nc.vector.memset(raw_scales[:].bitcast(I32), 0)
+        nc.vector.memset(warm[:], 0.0)
+        x_rows = xT.rearrange("(p i) t -> p i t", i=PACK)
+        nc.sync.dma_start(out=offsets[:], in_=offs)
+        nc.scalar.dma_start(out=raw_words[:].bitcast(I32), in_=w_words[0].bitcast(I32))
+        nc.sync.dma_start(out=planes[0][:], in_=x_rows[:, 0, :])
+        for q in range(4):
+            nc.scalar.dma_start(out=raw_scales[32 * q : 32 * q + 4, :].bitcast(I32), in_=w_scales[0, 4 * q : 4 * q + 4, :].bitcast(I32))
+        nc.sync.dma_start(out=weights[:, 0:J], in_=wgt[:, 0:J])
+        nc.sync.dma_start(out=weights[:, J:], in_=wgt[:, J:])
+        for i in range(1, PACK):
+            nc.sync.dma_start(out=planes[i][:], in_=x_rows[:, i, :])
+        nc.scalar.dma_start(out=bias[:], in_=b.rearrange("(p t) -> p t", t=PACK))
+        nc.scalar.activation(out=warm2[:], in_=warm[:], func=GELU)
+
+        w_codes = keep.tile([P, 2 * N], U8, name="w_codes", align_bytes=64)
+        w_plane = keep.tile([P, N], U8, name="w_plane", align_bytes=64)
+        nc.vector.tensor_copy(
+            out=w_codes[:].rearrange("p (t m e) -> p t m e", t=PACK, e=2),
+            in_=raw_words[:].rearrange("p (m t e) -> p t m e", t=PACK, e=2),
+        )
+        nc.vector.tensor_copy(
+            out=w_plane[:].rearrange("p (t m) -> p t m", t=PACK),
+            in_=raw_scales[:].rearrange("p (m t) -> p t m", t=PACK),
+        )
+
+        def gather(dst, i, first, width):
+            picks = offsets[:, first // LIST_ROWS : (first + width) // LIST_ROWS]
+            nc.vector.tensor_tensor(dst, planes[i][:].indirect(picks), weights[:, first : first + width], MULT)
+
+        units = [(j0, width, c) for j0, width in CHUNKS for c in range(PICKS)]
+        rounded = {}
+        for j0, width, c in units:
+            rounded[j0, c] = keep.tile([P, width, PACK], BF16, name="rounded%d_%d" % (j0, c), align_bytes=64)
+
+        early = [keep.tile([P, 2, J], F32, name="early%d" % c) for c in range(PICKS)]
+        for i in range(2):
+            for c in range(PICKS):
+                gather(early[c][:, i, :], i, c * J, J)
+        for j0, width, c in units:
+            nc.scalar.copy(out=rounded[j0, c][:, :, 0:2], in_=early[c][:, :, j0 : j0 + width].rearrange("p i j -> p j i"))
+
+        y_plane = keep.tile([P, J], U8, name="y_plane", align_bytes=64)
+        out_rows = out_0.rearrange("(p t) j -> p t j", t=PACK)
+        out_words = out_1[0].rearrange("p j i -> p (j i)").bitcast(I32)
+        sums = {}
+        best = {}
+
+        def late_gather(j0, width, c):
+            late = ring.tile([P, 2, width], F32, name="late", tag="late")
+            for i in range(2):
+                gather(late[:, i, :], 2 + i, c * J + j0, width)
+            nc.scalar.copy(out=rounded[j0, c][:, :, 2:4], in_=late[:].rearrange("p i j -> p j i"))
+
+        def project(j0, width, c):
+            codes = keep.tile([P, width], U32, name="codes%d_%d" % (j0, c), align_bytes=64)
+            scales = keep.tile([P, width], U8, name="scales%d_%d" % (j0, c), align_bytes=64)
+            nc.vector.quantize_mx(out=codes[:].bitcast(FP8X4), scales=scales[:], in_=rounded[j0, c][:].rearrange("p j i -> p (j i)"))
+            per_bank = BANK // width
+            banks = []
+            for t in range(PACK):
+                if t % per_bank == 0:
+                    banks.append(psum.tile([P, BANK], F32, name="bank", tag="bank"))
+                at = t % per_bank * width
+                nc.tensor.matmul_mx(
+                    out=banks[-1][:, at : at + width],
+                    lhsT=w_codes[:, 2 * P * t : 2 * P * (t + 1)].bitcast(FP4X4),
+                    lhsT_scale=w_plane[:, P * t : P * (t + 1)],
+                    rhs=codes[:].bitcast(FP8X4),
+                    rhs_scale=scales[:],
+                    start=True,
+                    stop=True,
+                )
+            sums[j0, c] = banks
+
+        def pool_picks(j0, width, c):
+            for n, bank in enumerate(sums[j0, c]):
+                new = keep.tile([P, BANK], F32, name="best%d_%d_%d" % (j0, c, n))
+                if c == 0:
+                    nc.scalar.copy(out=new[:], in_=bank[:])
+                else:
+                    nc.vector.tensor_tensor(new[:], bank[:], best[j0, n][:], MAX)
+                best[j0, n] = new
+
+        def finish(j0, width):
+            per_bank = BANK // width
+            y = keep.tile([P, PACK, width], F32, name="y%d" % j0)
+            for t in range(PACK):
+                at = t % per_bank * width
+                nc.scalar.activation(out=y[:, t, :], in_=best[j0, t // per_bank][:, at : at + width], func=GELU, bias=bias[:, t : t + 1])
+            nc.sync.dma_start(out=out_rows[:, :, j0 : j0 + width], in_=y[:])
+            y_rounded = keep.tile([P, width, PACK], BF16, name="y_rounded%d" % j0, align_bytes=64)
+            dst = y_rounded[:].rearrange("p (a e) t -> p a t e", e=4)
+            src = y[:].rearrange("p t (a e) -> p a t e", e=4)
+            if j0 + width == J:
+                nc.vector.tensor_copy(out=dst, in_=src)
+            else:
+                nc.scalar.copy(out=dst, in_=src)
+            return y_rounded
+
+        def hand_on(j0, width, y_rounded):
+            y_codes = keep.tile([P, width], U32, name="y_codes%d" % j0, align_bytes=64)
+            nc.vector.quantize_mx(out=y_codes[:].bitcast(FP8X4), scales=y_plane[:, j0 : j0 + width], in_=y_rounded[:].rearrange("p j t -> p (j t)"))
+            nc.sync.dma_start(out=out_words[:, j0 : j0 + width], in_=y_codes[:].bitcast(I32))
+
+        waiting = []
+        for s in range(len(units) + 3):
+            if s < len(units):
+                late_gather(*units[s])
+            if 1 <= s <= len(units):
+                project(*units[s - 1])
+            for item in waiting:
+                hand_on(*item)
+            waiting = []
+            if 2 <= s <= len(units) + 1:
+                j0, width, c = units[s - 2]
+                pool_picks(j0, width, c)
+                if c == PICKS - 1:
+                    waiting.append((j0, width, finish(j0, width)))
+        for q in range(4):
+            queue = nc.scalar if q % 2 else nc.sync
+            queue.dma_start(out=out_2[0, 4 * q : 4 * q + 4, :].bitcast(I32), in_=y_plane[32 * q : 32 * q + 4, :].bitcast(I32))

@@ -20,21 +20,20 @@ GELU = mybir.ActivationFunctionType.Gelu_apprx_tanh
 
 P = 128
 PACK = 4
-BANK = 512
+PIECE = 128
+HALF = 256
 LIST_ROWS = 16
-CHUNKS = ((0, 256), (256, 256))
 
 
 def tile_list_max_geluP_kernel(tc, xT, wgt, w_words, w_scales, b, offs, out_0, out_1, out_2):
     nc = tc.nc
     with ExitStack() as ctx:
         keep = ctx.enter_context(tc.tile_pool(name="keep", bufs=1))
-        ring = ctx.enter_context(tc.tile_pool(name="ring", bufs=3))
         psum = ctx.enter_context(tc.psum_pool(name="psum", bufs=8))
 
         offsets = keep.tile([P, PICKS * J // LIST_ROWS], U16, name="offsets")
         planes = [keep.tile([P, T], F32, name="plane%d" % i) for i in range(PACK)]
-        weights = keep.tile([P, PICKS * J], F32, name="weights")
+        weights = [keep.tile([P, J], F32, name="weights%d" % c) for c in range(PICKS)]
         raw_words = keep.tile([P, 2 * N], U8, name="raw_words")
         raw_scales = keep.tile([P, N], U8, name="raw_scales")
         bias = keep.tile([P, PACK], F32, name="bias")
@@ -47,12 +46,13 @@ def tile_list_max_geluP_kernel(tc, xT, wgt, w_words, w_scales, b, offs, out_0, o
         nc.sync.dma_start(out=offsets[:], in_=offs)
         nc.scalar.dma_start(out=raw_words[:].bitcast(I32), in_=w_words[0].bitcast(I32))
         nc.sync.dma_start(out=planes[0][:], in_=x_rows[:, 0, :])
+        for c in range(2):
+            nc.sync.dma_start(out=weights[c][:], in_=wgt[:, c * J : (c + 1) * J])
         for q in range(4):
-            nc.scalar.dma_start(out=raw_scales[32 * q : 32 * q + 4, :].bitcast(I32), in_=w_scales[0, 4 * q : 4 * q + 4, :].bitcast(I32))
-        nc.sync.dma_start(out=weights[:, 0:J], in_=wgt[:, 0:J])
-        nc.sync.dma_start(out=weights[:, J:], in_=wgt[:, J:])
+            nc.sync.dma_start(out=raw_scales[32 * q : 32 * q + 4, :].bitcast(I32), in_=w_scales[0, 4 * q : 4 * q + 4, :].bitcast(I32))
         for i in range(1, PACK):
             nc.sync.dma_start(out=planes[i][:], in_=x_rows[:, i, :])
+        nc.sync.dma_start(out=weights[2][:], in_=wgt[:, 2 * J :])
         nc.scalar.dma_start(out=bias[:], in_=b.rearrange("(p t) -> p t", t=PACK))
         nc.scalar.activation(out=warm2[:], in_=warm[:], func=GELU)
 
@@ -62,104 +62,91 @@ def tile_list_max_geluP_kernel(tc, xT, wgt, w_words, w_scales, b, offs, out_0, o
             out=w_codes[:].rearrange("p (t m e) -> p t m e", t=PACK, e=2),
             in_=raw_words[:].rearrange("p (m t e) -> p t m e", t=PACK, e=2),
         )
+
+        def gather(dst, i, c, j0, width):
+            first = c * J + j0
+            picks = offsets[:, first // LIST_ROWS : (first + width) // LIST_ROWS]
+            nc.vector.tensor_tensor(dst, planes[i][:].indirect(picks), weights[c][:, j0 : j0 + width], MULT)
+
+        def quantize(rounded, width, name):
+            codes = keep.tile([P, width], U32, name="codes" + name, tag="codes" + name, align_bytes=64)
+            scales = keep.tile([P, width], U8, name="scales" + name, align_bytes=64)
+            nc.vector.quantize_mx(out=codes[:].bitcast(FP8X4), scales=scales[:], in_=rounded[:].rearrange("p j i -> p (j i)"))
+            return codes, scales
+
+        def project(operand, at):
+            codes, scales = operand
+            bank = psum.tile([P, PACK, PIECE], F32, name="bank", tag="bank")
+            for t in range(PACK):
+                nc.tensor.matmul_mx(
+                    out=bank[:, t, :],
+                    lhsT=w_codes[:, 2 * P * t : 2 * P * (t + 1)].bitcast(FP4X4),
+                    lhsT_scale=w_plane[:, P * t : P * (t + 1)],
+                    rhs=codes[:, at : at + PIECE].bitcast(FP8X4),
+                    rhs_scale=scales[:, at : at + PIECE],
+                    start=True,
+                    stop=True,
+                )
+            return bank
+
+        rounded = [keep.tile([P, J, PACK], BF16, name="rounded%d" % c, tag="rounded%d" % c, align_bytes=64) for c in range(2)]
+        for pair in range(2):
+            picked = [keep.tile([P, 2, J], F32, name="picked%d_%d" % (pair, c)) for c in range(2)]
+            for i in range(2):
+                for c in range(2):
+                    gather(picked[c][:, i, :], 2 * pair + i, c, 0, J)
+            for c in range(2):
+                nc.scalar.copy(out=rounded[c][:, :, 2 * pair : 2 * pair + 2], in_=picked[c][:].rearrange("p i j -> p j i"))
         nc.vector.tensor_copy(
             out=w_plane[:].rearrange("p (t m) -> p t m", t=PACK),
             in_=raw_scales[:].rearrange("p (m t) -> p t m", t=PACK),
         )
+        operands = [quantize(rounded[c], J, "%d" % c) for c in range(2)]
 
-        def gather(dst, i, first, width):
-            picks = offsets[:, first // LIST_ROWS : (first + width) // LIST_ROWS]
-            nc.vector.tensor_tensor(dst, planes[i][:].indirect(picks), weights[:, first : first + width], MULT)
+        first = []
+        for k in range(J // PIECE):
+            bank = project(operands[0], k * PIECE)
+            held = keep.tile([P, PACK, PIECE], F32, name="first%d" % k)
+            nc.scalar.copy(out=held[:], in_=bank[:])
+            first.append(held)
 
-        units = [(j0, width, c) for j0, width in CHUNKS for c in range(PICKS)]
-        rounded = {}
-        for j0, width, c in units:
-            rounded[j0, c] = keep.tile([P, width, PACK], BF16, name="rounded%d_%d" % (j0, c), align_bytes=64)
-
-        early = [keep.tile([P, 2, J], F32, name="early%d" % c) for c in range(PICKS)]
-        for i in range(2):
-            for c in range(PICKS):
-                gather(early[c][:, i, :], i, c * J, J)
-        for j0, width, c in units:
-            nc.scalar.copy(out=rounded[j0, c][:, :, 0:2], in_=early[c][:, :, j0 : j0 + width].rearrange("p i j -> p j i"))
+        last = []
+        for h in range(J // HALF):
+            picked = keep.tile([P, PACK, HALF], F32, name="picked_last%d" % h, tag=("picked_last0", "rounded1")[h], align_bytes=64)
+            for i in range(PACK):
+                gather(picked[:, i, :], i, 2, h * HALF, HALF)
+            whole = keep.tile([P, HALF, PACK], BF16, name="rounded_last%d" % h, tag=("rounded_last0", "codes0")[h], align_bytes=64)
+            nc.scalar.copy(out=whole[:].rearrange("p (a e) i -> p a i e", e=4), in_=picked[:].rearrange("p i (a e) -> p a i e", e=4))
+            last.append(quantize(whole, HALF, "_last%d" % h))
 
         y_plane = keep.tile([P, J], U8, name="y_plane", align_bytes=64)
         out_rows = out_0.rearrange("(p t) j -> p t j", t=PACK)
         out_words = out_1[0].rearrange("p j i -> p (j i)").bitcast(I32)
-        sums = {}
-        best = {}
-
-        def late_gather(j0, width, c):
-            late = ring.tile([P, 2, width], F32, name="late", tag="late")
-            for i in range(2):
-                gather(late[:, i, :], 2 + i, c * J + j0, width)
-            nc.scalar.copy(out=rounded[j0, c][:, :, 2:4], in_=late[:].rearrange("p i j -> p j i"))
-
-        def project(j0, width, c):
-            codes = keep.tile([P, width], U32, name="codes%d_%d" % (j0, c), align_bytes=64)
-            scales = keep.tile([P, width], U8, name="scales%d_%d" % (j0, c), align_bytes=64)
-            nc.vector.quantize_mx(out=codes[:].bitcast(FP8X4), scales=scales[:], in_=rounded[j0, c][:].rearrange("p j i -> p (j i)"))
-            per_bank = BANK // width
-            banks = []
+        of_two = {}
+        for k in range(J // PIECE):
+            j0 = k * PIECE
+            if k % 2 == 0:
+                for n in (k, k + 1):
+                    second = project(operands[1], n * PIECE)
+                    of_two[n] = keep.tile([P, PACK, PIECE], F32, name="of_two%d" % n)
+                    nc.vector.tensor_tensor(of_two[n][:], second[:], first[n][:], MAX)
+            third = project(last[j0 // HALF], j0 % HALF)
+            of_three = keep.tile([P, PACK, PIECE], F32, name="of_three%d" % k)
+            nc.vector.tensor_tensor(of_three[:], third[:], of_two[k][:], MAX)
+            y = keep.tile([P, PACK, PIECE], F32, name="y%d" % k)
             for t in range(PACK):
-                if t % per_bank == 0:
-                    banks.append(psum.tile([P, BANK], F32, name="bank", tag="bank"))
-                at = t % per_bank * width
-                nc.tensor.matmul_mx(
-                    out=banks[-1][:, at : at + width],
-                    lhsT=w_codes[:, 2 * P * t : 2 * P * (t + 1)].bitcast(FP4X4),
-                    lhsT_scale=w_plane[:, P * t : P * (t + 1)],
-                    rhs=codes[:].bitcast(FP8X4),
-                    rhs_scale=scales[:],
-                    start=True,
-                    stop=True,
-                )
-            sums[j0, c] = banks
-
-        def pool_picks(j0, width, c):
-            for n, bank in enumerate(sums[j0, c]):
-                new = keep.tile([P, BANK], F32, name="best%d_%d_%d" % (j0, c, n))
-                if c == 0:
-                    nc.scalar.copy(out=new[:], in_=bank[:])
-                else:
-                    nc.vector.tensor_tensor(new[:], bank[:], best[j0, n][:], MAX)
-                best[j0, n] = new
-
-        def finish(j0, width):
-            per_bank = BANK // width
-            y = keep.tile([P, PACK, width], F32, name="y%d" % j0)
-            for t in range(PACK):
-                at = t % per_bank * width
-                nc.scalar.activation(out=y[:, t, :], in_=best[j0, t // per_bank][:, at : at + width], func=GELU, bias=bias[:, t : t + 1])
-            nc.sync.dma_start(out=out_rows[:, :, j0 : j0 + width], in_=y[:])
-            y_rounded = keep.tile([P, width, PACK], BF16, name="y_rounded%d" % j0, align_bytes=64)
+                nc.scalar.activation(out=y[:, t, :], in_=of_three[:, t, :], func=GELU, bias=bias[:, t : t + 1])
+            nc.sync.dma_start(out=out_rows[:, :, j0 : j0 + PIECE], in_=y[:])
+            y_rounded = keep.tile([P, PIECE, PACK], BF16, name="y_rounded%d" % k, align_bytes=64)
             dst = y_rounded[:].rearrange("p (a e) t -> p a t e", e=4)
             src = y[:].rearrange("p t (a e) -> p a t e", e=4)
-            if j0 + width == J:
+            if k >= 2:
                 nc.vector.tensor_copy(out=dst, in_=src)
             else:
                 nc.scalar.copy(out=dst, in_=src)
-            return y_rounded
-
-        def hand_on(j0, width, y_rounded):
-            y_codes = keep.tile([P, width], U32, name="y_codes%d" % j0, align_bytes=64)
-            nc.vector.quantize_mx(out=y_codes[:].bitcast(FP8X4), scales=y_plane[:, j0 : j0 + width], in_=y_rounded[:].rearrange("p j t -> p (j t)"))
-            nc.sync.dma_start(out=out_words[:, j0 : j0 + width], in_=y_codes[:].bitcast(I32))
-
-        waiting = []
-        for s in range(len(units) + 3):
-            if s < len(units):
-                late_gather(*units[s])
-            if 1 <= s <= len(units):
-                project(*units[s - 1])
-            for item in waiting:
-                hand_on(*item)
-            waiting = []
-            if 2 <= s <= len(units) + 1:
-                j0, width, c = units[s - 2]
-                pool_picks(j0, width, c)
-                if c == PICKS - 1:
-                    waiting.append((j0, width, finish(j0, width)))
+            y_codes = keep.tile([P, PIECE], U32, name="y_codes%d" % k, align_bytes=64)
+            nc.vector.quantize_mx(out=y_codes[:].bitcast(FP8X4), scales=y_plane[:, j0 : j0 + PIECE], in_=y_rounded[:].rearrange("p j t -> p (j t)"))
+            nc.sync.dma_start(out=out_words[:, j0 : j0 + PIECE], in_=y_codes[:].bitcast(I32))
         for q in range(4):
             queue = nc.scalar if q % 2 else nc.sync
             queue.dma_start(out=out_2[0, 4 * q : 4 * q + 4, :].bitcast(I32), in_=y_plane[32 * q : 32 * q + 4, :].bitcast(I32))

@@ -23,6 +23,7 @@ PACK = 4
 PIECE = 128
 HALF = 256
 LIST_ROWS = 16
+SEED = 64
 
 
 def tile_list_max_geluP_kernel(tc, xT, wgt, w_words, w_scales, b, offs, out_0, out_1, out_2):
@@ -33,34 +34,47 @@ def tile_list_max_geluP_kernel(tc, xT, wgt, w_words, w_scales, b, offs, out_0, o
 
         offsets = keep.tile([P, PICKS * J // LIST_ROWS], U16, name="offsets")
         planes = [keep.tile([P, T], F32, name="plane%d" % i) for i in range(PACK)]
-        weights = [keep.tile([P, J], F32, name="weights%d" % c) for c in range(PICKS)]
+        weights = [keep.tile([P, J], F32, name="weights%d" % c, align_bytes=64) for c in range(PICKS)]
+        seeds = keep.tile([P, SEED], F32, name="seeds", align_bytes=64)
+        turned = keep.tile([P, SEED], F32, name="turned", align_bytes=64)
+        spread = [keep.tile([P, J], F32, name="spread%d" % c, align_bytes=64) for c in range(2)]
         raw_words = keep.tile([P, 2 * N], U8, name="raw_words")
         raw_scales = keep.tile([P, N], U8, name="raw_scales")
         bias = keep.tile([P, PACK], F32, name="bias")
         warm = keep.tile([P, 8], F32, name="warm")
         warm2 = keep.tile([P, 8], F32, name="warm2")
 
-        nc.vector.memset(raw_scales[:].bitcast(I32), 0)
-        nc.vector.memset(warm[:], 0.0)
+        nc.gpsimd.memset(warm[:], 0.0)
+        nc.gpsimd.memset(raw_scales[:].bitcast(I32), 0)
         x_rows = xT.rearrange("(p i) t -> p i t", i=PACK)
-        nc.sync.dma_start(out=offsets[:], in_=offs)
-        nc.scalar.dma_start(out=raw_words[:].bitcast(I32), in_=w_words[0].bitcast(I32))
+        seed_rows = wgt.rearrange("(h r) c -> h r c", r=LIST_ROWS)[:, 0, 0 : 2 * J].rearrange("h (s c) -> h s c", c=SEED)
+        nc.sync.dma_start(out=seeds[:], in_=seed_rows)
+        nc.sync.dma_start(out=raw_words[:].bitcast(I32), in_=w_words[0].bitcast(I32))
         nc.sync.dma_start(out=planes[0][:], in_=x_rows[:, 0, :])
-        for c in range(2):
-            nc.sync.dma_start(out=weights[c][:], in_=wgt[:, c * J : (c + 1) * J])
+        nc.sync.dma_start(out=offsets[:], in_=offs)
+        nc.sync.dma_start(out=planes[1][:], in_=x_rows[:, 1, :])
         for q in range(4):
             nc.sync.dma_start(out=raw_scales[32 * q : 32 * q + 4, :].bitcast(I32), in_=w_scales[0, 4 * q : 4 * q + 4, :].bitcast(I32))
-        for i in range(1, PACK):
+        for i in range(2, PACK):
             nc.sync.dma_start(out=planes[i][:], in_=x_rows[:, i, :])
         nc.sync.dma_start(out=weights[2][:], in_=wgt[:, 2 * J :])
-        nc.scalar.dma_start(out=bias[:], in_=b.rearrange("(p t) -> p t", t=PACK))
+        nc.sync.dma_start(out=bias[:], in_=b.rearrange("(p t) -> p t", t=PACK))
         nc.scalar.activation(out=warm2[:], in_=warm[:], func=GELU)
+
+        for blk in range(SEED // 32):
+            nc.vector.transpose(turned[:, 32 * blk : 32 * blk + 32], seeds[:, 32 * blk : 32 * blk + 32])
+        by_seed = turned[:].rearrange("p (g s) -> p s g", s=LIST_ROWS)
+        for c in range(2):
+            src = by_seed[:, 8 * c : 8 * c + 8, :].unsqueeze(3).to_broadcast([P, 8, 4, LIST_ROWS])
+            nc.scalar.copy(out=spread[c][:].rearrange("p (s g r) -> p s g r", g=4, r=LIST_ROWS), in_=src)
 
         w_codes = keep.tile([P, 2 * N], U8, name="w_codes", align_bytes=64)
         w_plane = keep.tile([P, N], U8, name="w_plane", align_bytes=64)
+        for c in range(2):
+            nc.vector.transpose(weights[c][:], spread[c][:])
         nc.vector.tensor_copy(
-            out=w_codes[:].rearrange("p (t m e) -> p t m e", t=PACK, e=2),
-            in_=raw_words[:].rearrange("p (m t e) -> p t m e", t=PACK, e=2),
+            out=w_codes[:].bitcast(U16).rearrange("p (t m) -> p t m", t=PACK),
+            in_=raw_words[:].bitcast(U16).rearrange("p (m t) -> p t m", t=PACK),
         )
 
         def gather(dst, i, c, j0, width):
@@ -89,50 +103,64 @@ def tile_list_max_geluP_kernel(tc, xT, wgt, w_words, w_scales, b, offs, out_0, o
                 )
             return bank
 
-        rounded = [keep.tile([P, J, PACK], BF16, name="rounded%d" % c, tag="rounded%d" % c, align_bytes=64) for c in range(2)]
-        for pair in range(2):
-            picked = [keep.tile([P, 2, J], F32, name="picked%d_%d" % (pair, c)) for c in range(2)]
-            for i in range(2):
-                for c in range(2):
-                    gather(picked[c][:, i, :], 2 * pair + i, c, 0, J)
+        units = [(c, h) for c in range(2) for h in range(2)]
+        rounded = {u: keep.tile([P, HALF, PACK], BF16, name="rounded%d_%d" % u, align_bytes=64) for u in units}
+        early = [keep.tile([P, 2, J], F32, name="early%d" % c) for c in range(2)]
+        ring = keep.tile([P, 8, HALF], F32, name="ring")
+        late = {u: ring[:, 2 * n : 2 * n + 2, :] for n, u in enumerate(units)}
+        for i in range(2):
             for c in range(2):
-                nc.scalar.copy(out=rounded[c][:, :, 2 * pair : 2 * pair + 2], in_=picked[c][:].rearrange("p i j -> p j i"))
+                gather(early[c][:, i, :], i, c, 0, J)
+        for c, h in units:
+            nc.scalar.copy(out=rounded[c, h][:, :, 0:2], in_=early[c][:, :, h * HALF : (h + 1) * HALF].rearrange("p i j -> p j i"))
+        for c, h in units:
+            gather(late[c, h][:, 0, :], 2, c, h * HALF, HALF)
         nc.vector.tensor_copy(
             out=w_plane[:].rearrange("p (t m) -> p t m", t=PACK),
             in_=raw_scales[:].rearrange("p (m t) -> p t m", t=PACK),
         )
-        operands = [quantize(rounded[c], J, "%d" % c) for c in range(2)]
-
+        operands = {}
         first = []
-        for k in range(J // PIECE):
-            bank = project(operands[0], k * PIECE)
+        for c, h in units:
+            gather(late[c, h][:, 1, :], 3, c, h * HALF, HALF)
+            nc.scalar.copy(out=rounded[c, h][:, :, 2:4], in_=late[c, h].rearrange("p i j -> p j i"))
+            operands[c, h] = quantize(rounded[c, h], HALF, "%d_%d" % (c, h))
+        def hold_first(k):
+            bank = project(operands[0, k // 2], (k % 2) * PIECE)
             held = keep.tile([P, PACK, PIECE], F32, name="first%d" % k)
             nc.scalar.copy(out=held[:], in_=bank[:])
             first.append(held)
 
-        last = []
-        for h in range(J // HALF):
-            picked = keep.tile([P, PACK, HALF], F32, name="picked_last%d" % h, tag=("picked_last0", "rounded1")[h], align_bytes=64)
-            for i in range(PACK):
-                gather(picked[:, i, :], i, 2, h * HALF, HALF)
-            whole = keep.tile([P, HALF, PACK], BF16, name="rounded_last%d" % h, tag=("rounded_last0", "codes0")[h], align_bytes=64)
-            nc.scalar.copy(out=whole[:].rearrange("p (a e) i -> p a i e", e=4), in_=picked[:].rearrange("p i (a e) -> p a i e", e=4))
-            last.append(quantize(whole, HALF, "_last%d" % h))
+        whole = [keep.tile([P, HALF, PACK], BF16, name="rounded_last%d" % h, align_bytes=64) for h in range(2)]
+        for i in range(PACK):
+            gather(ring[:, i, :], i, 2, 0, HALF)
+        hold_first(0)
+        hold_first(1)
+        for i in (2, 3):
+            gather(ring[:, 2 + i, :], i, 2, HALF, HALF)
+        nc.scalar.copy(out=whole[0][:].rearrange("p (a e) i -> p a i e", e=4), in_=ring[:, 0:4, :].rearrange("p i (a e) -> p a i e", e=4))
+        operands[2, 0] = quantize(whole[0], HALF, "_last0")
+        for i in (0, 1):
+            gather(ring[:, i, :], i, 2, HALF, HALF)
+        hold_first(2)
+        hold_first(3)
+        nc.scalar.copy(
+            out=whole[1][:].rearrange("p (a e) (u i) -> p a u i e", e=4, u=2),
+            in_=ring[:].rearrange("p (u v) (a e) -> p a u v e", u=2, e=4)[:, :, :, 0:2, :],
+        )
+        operands[2, 1] = quantize(whole[1], HALF, "_last1")
 
         y_plane = keep.tile([P, J], U8, name="y_plane", align_bytes=64)
         out_rows = out_0.rearrange("(p t) j -> p t j", t=PACK)
         out_words = out_1[0].rearrange("p j i -> p (j i)").bitcast(I32)
-        of_two = {}
         for k in range(J // PIECE):
             j0 = k * PIECE
-            if k % 2 == 0:
-                for n in (k, k + 1):
-                    second = project(operands[1], n * PIECE)
-                    of_two[n] = keep.tile([P, PACK, PIECE], F32, name="of_two%d" % n)
-                    nc.vector.tensor_tensor(of_two[n][:], second[:], first[n][:], MAX)
-            third = project(last[j0 // HALF], j0 % HALF)
+            second = project(operands[1, k // 2], j0 % HALF)
+            of_two = keep.tile([P, PACK, PIECE], F32, name="of_two%d" % k)
+            nc.vector.tensor_tensor(of_two[:], second[:], first[k][:], MAX)
+            third = project(operands[2, k // 2], j0 % HALF)
             of_three = keep.tile([P, PACK, PIECE], F32, name="of_three%d" % k)
-            nc.vector.tensor_tensor(of_three[:], third[:], of_two[k][:], MAX)
+            nc.vector.tensor_tensor(of_three[:], third[:], of_two[:], MAX)
             y = keep.tile([P, PACK, PIECE], F32, name="y%d" % k)
             for t in range(PACK):
                 nc.scalar.activation(out=y[:, t, :], in_=of_three[:, t, :], func=GELU, bias=bias[:, t : t + 1])
@@ -140,7 +168,7 @@ def tile_list_max_geluP_kernel(tc, xT, wgt, w_words, w_scales, b, offs, out_0, o
             y_rounded = keep.tile([P, PIECE, PACK], BF16, name="y_rounded%d" % k, align_bytes=64)
             dst = y_rounded[:].rearrange("p (a e) t -> p a t e", e=4)
             src = y[:].rearrange("p t (a e) -> p a t e", e=4)
-            if k >= 2:
+            if k >= 3:
                 nc.vector.tensor_copy(out=dst, in_=src)
             else:
                 nc.scalar.copy(out=dst, in_=src)

@@ -66,7 +66,11 @@ def tile_list_max_geluP_kernel(tc, xT, wgt, w_words, w_scales, b, offs, out_0, o
         by_seed = turned[:].rearrange("p (g s) -> p s g", s=LIST_ROWS)
         for c in range(2):
             src = by_seed[:, 8 * c : 8 * c + 8, :].unsqueeze(3).to_broadcast([P, 8, 4, LIST_ROWS])
-            nc.scalar.copy(out=spread[c][:].rearrange("p (s g r) -> p s g r", g=4, r=LIST_ROWS), in_=src)
+            dst = spread[c][:].rearrange("p (s g r) -> p s g r", g=4, r=LIST_ROWS)
+            if c == 0:
+                nc.vector.tensor_copy(out=dst, in_=src)
+            else:
+                nc.scalar.copy(out=dst, in_=src)
 
         w_codes = keep.tile([P, 2 * N], U8, name="w_codes", align_bytes=64)
         w_plane = keep.tile([P, N], U8, name="w_plane", align_bytes=64)
@@ -103,78 +107,85 @@ def tile_list_max_geluP_kernel(tc, xT, wgt, w_words, w_scales, b, offs, out_0, o
                 )
             return bank
 
-        units = [(c, h) for c in range(2) for h in range(2)]
-        rounded = {u: keep.tile([P, HALF, PACK], BF16, name="rounded%d_%d" % u, align_bytes=64) for u in units}
-        early = [keep.tile([P, 2, J], F32, name="early%d" % c) for c in range(2)]
-        ring = keep.tile([P, 8, HALF], F32, name="ring")
-        late = {u: ring[:, 2 * n : 2 * n + 2, :] for n, u in enumerate(units)}
-        for i in range(2):
-            for c in range(2):
-                gather(early[c][:, i, :], i, c, 0, J)
-        for c, h in units:
-            nc.scalar.copy(out=rounded[c, h][:, :, 0:2], in_=early[c][:, :, h * HALF : (h + 1) * HALF].rearrange("p i j -> p j i"))
-        for c, h in units:
-            gather(late[c, h][:, 0, :], 2, c, h * HALF, HALF)
-        nc.vector.tensor_copy(
-            out=w_plane[:].rearrange("p (t m) -> p t m", t=PACK),
-            in_=raw_scales[:].rearrange("p (m t) -> p t m", t=PACK),
-        )
+        picked = [keep.tile([P, PACK, J], F32, name="picked%d" % c) for c in range(2)]
         operands = {}
-        first = []
-        for c, h in units:
-            gather(late[c, h][:, 1, :], 3, c, h * HALF, HALF)
-            nc.scalar.copy(out=rounded[c, h][:, :, 2:4], in_=late[c, h].rearrange("p i j -> p j i"))
-            operands[c, h] = quantize(rounded[c, h], HALF, "%d_%d" % (c, h))
+        first = {}
+        of_two = {}
+        of_three = {}
+
+        def round_unit(c, h, rows):
+            rounded = keep.tile([P, HALF, PACK], BF16, name="rounded%d_%d" % (c, h), align_bytes=64)
+            nc.scalar.copy(out=rounded[:].rearrange("p (a e) i -> p a i e", e=4), in_=rows.rearrange("p i (a e) -> p a i e", e=4))
+            operands[c, h] = quantize(rounded, HALF, "%d_%d" % (c, h))
+
         def hold_first(k):
             bank = project(operands[0, k // 2], (k % 2) * PIECE)
-            held = keep.tile([P, PACK, PIECE], F32, name="first%d" % k)
-            nc.scalar.copy(out=held[:], in_=bank[:])
-            first.append(held)
+            first[k] = keep.tile([P, PACK, PIECE], F32, name="first%d" % k)
+            nc.scalar.copy(out=first[k][:], in_=bank[:])
 
-        whole = [keep.tile([P, HALF, PACK], BF16, name="rounded_last%d" % h, align_bytes=64) for h in range(2)]
-        for i in range(PACK):
-            gather(ring[:, i, :], i, 2, 0, HALF)
-        hold_first(0)
-        hold_first(1)
-        for i in (2, 3):
-            gather(ring[:, 2 + i, :], i, 2, HALF, HALF)
-        nc.scalar.copy(out=whole[0][:].rearrange("p (a e) i -> p a i e", e=4), in_=ring[:, 0:4, :].rearrange("p i (a e) -> p a i e", e=4))
-        operands[2, 0] = quantize(whole[0], HALF, "_last0")
-        for i in (0, 1):
-            gather(ring[:, i, :], i, 2, HALF, HALF)
-        hold_first(2)
-        hold_first(3)
-        nc.scalar.copy(
-            out=whole[1][:].rearrange("p (a e) (u i) -> p a u i e", e=4, u=2),
-            in_=ring[:].rearrange("p (u v) (a e) -> p a u v e", u=2, e=4)[:, :, :, 0:2, :],
-        )
-        operands[2, 1] = quantize(whole[1], HALF, "_last1")
+        def max_of_two(k):
+            second = project(operands[1, k // 2], (k % 2) * PIECE)
+            of_two[k] = keep.tile([P, PACK, PIECE], F32, name="of_two%d" % k)
+            nc.vector.tensor_tensor(of_two[k][:], second[:], first[k][:], MAX)
+
+        def max_of_three(k):
+            third = project(operands[2, k // 2], (k % 2) * PIECE)
+            of_three[k] = keep.tile([P, PACK, PIECE], F32, name="of_three%d" % k)
+            nc.vector.tensor_tensor(of_three[k][:], third[:], of_two[k][:], MAX)
 
         y_plane = keep.tile([P, J], U8, name="y_plane", align_bytes=64)
         out_rows = out_0.rearrange("(p t) j -> p t j", t=PACK)
         out_words = out_1[0].rearrange("p j i -> p (j i)").bitcast(I32)
-        for k in range(J // PIECE):
+
+        def finish(k):
             j0 = k * PIECE
-            second = project(operands[1, k // 2], j0 % HALF)
-            of_two = keep.tile([P, PACK, PIECE], F32, name="of_two%d" % k)
-            nc.vector.tensor_tensor(of_two[:], second[:], first[k][:], MAX)
-            third = project(operands[2, k // 2], j0 % HALF)
-            of_three = keep.tile([P, PACK, PIECE], F32, name="of_three%d" % k)
-            nc.vector.tensor_tensor(of_three[:], third[:], of_two[:], MAX)
             y = keep.tile([P, PACK, PIECE], F32, name="y%d" % k)
             for t in range(PACK):
-                nc.scalar.activation(out=y[:, t, :], in_=of_three[:, t, :], func=GELU, bias=bias[:, t : t + 1])
+                nc.scalar.activation(out=y[:, t, :], in_=of_three[k][:, t, :], func=GELU, bias=bias[:, t : t + 1])
             nc.sync.dma_start(out=out_rows[:, :, j0 : j0 + PIECE], in_=y[:])
             y_rounded = keep.tile([P, PIECE, PACK], BF16, name="y_rounded%d" % k, align_bytes=64)
             dst = y_rounded[:].rearrange("p (a e) t -> p a t e", e=4)
             src = y[:].rearrange("p t (a e) -> p a t e", e=4)
-            if k >= 3:
+            if k >= 2:
                 nc.vector.tensor_copy(out=dst, in_=src)
             else:
                 nc.scalar.copy(out=dst, in_=src)
             y_codes = keep.tile([P, PIECE], U32, name="y_codes%d" % k, align_bytes=64)
             nc.vector.quantize_mx(out=y_codes[:].bitcast(FP8X4), scales=y_plane[:, j0 : j0 + PIECE], in_=y_rounded[:].rearrange("p j t -> p (j t)"))
             nc.sync.dma_start(out=out_words[:, j0 : j0 + PIECE], in_=y_codes[:].bitcast(I32))
+
+        for i in range(3):
+            for c in range(2):
+                gather(picked[c][:, i, :], i, c, 0, J)
+        nc.vector.tensor_copy(
+            out=w_plane[:].rearrange("p (t m) -> p t m", t=PACK),
+            in_=raw_scales[:].rearrange("p (m t) -> p t m", t=PACK),
+        )
+        for c in range(2):
+            for h in range(2):
+                gather(picked[c][:, 3, h * HALF : (h + 1) * HALF], 3, c, h * HALF, HALF)
+        for c in range(2):
+            for h in range(2):
+                round_unit(c, h, picked[c][:, :, h * HALF : (h + 1) * HALF])
+        for h in range(2):
+            for i in range(PACK):
+                gather(picked[h][:, i, 0:HALF], i, 2, h * HALF, HALF)
+        round_unit(2, 0, picked[0][:, :, 0:HALF])
+        for k in range(4):
+            hold_first(k)
+        for k in (0, 1):
+            max_of_two(k)
+        for k in (0, 1):
+            max_of_three(k)
+        round_unit(2, 1, picked[1][:, :, 0:HALF])
+        for k in (2, 3):
+            max_of_two(k)
+        for k in (0, 1):
+            finish(k)
+        for k in (2, 3):
+            max_of_three(k)
+        for k in (2, 3):
+            finish(k)
         for q in range(4):
             queue = nc.scalar if q % 2 else nc.sync
             queue.dma_start(out=out_2[0, 4 * q : 4 * q + 4, :].bitcast(I32), in_=y_plane[32 * q : 32 * q + 4, :].bitcast(I32))

@@ -23,7 +23,7 @@ PACK = 4
 PIECE = 128
 HALF = 256
 LIST_ROWS = 16
-SEED = 64
+SEED = 32
 
 
 def tile_list_max_geluP_kernel(tc, xT, wgt, w_words, w_scales, b, offs, out_0, out_1, out_2):
@@ -34,57 +34,51 @@ def tile_list_max_geluP_kernel(tc, xT, wgt, w_words, w_scales, b, offs, out_0, o
 
         offsets = keep.tile([P, PICKS * J // LIST_ROWS], U16, name="offsets")
         planes = [keep.tile([P, T], F32, name="plane%d" % i) for i in range(PACK)]
-        weights = [keep.tile([P, J], F32, name="weights%d" % c, align_bytes=64) for c in range(PICKS)]
+        weights = keep.tile([P, PICKS * J], F32, name="weights", align_bytes=64)
         seeds = keep.tile([P, SEED], F32, name="seeds", align_bytes=64)
         turned = keep.tile([P, SEED], F32, name="turned", align_bytes=64)
-        spread = [keep.tile([P, J], F32, name="spread%d" % c, align_bytes=64) for c in range(2)]
+        spread = keep.tile([P, J], F32, name="spread", align_bytes=64)
         raw_words = keep.tile([P, 2 * N], U8, name="raw_words")
         raw_scales = keep.tile([P, N], U8, name="raw_scales")
         bias = keep.tile([P, PACK], F32, name="bias")
         warm = keep.tile([P, 8], F32, name="warm")
         warm2 = keep.tile([P, 8], F32, name="warm2")
 
-        nc.gpsimd.memset(warm[:], 0.0)
-        nc.gpsimd.memset(raw_scales[:].bitcast(I32), 0)
+        nc.vector.memset(warm[:], 0.0)
+        nc.vector.memset(raw_scales[:].bitcast(I32), 0)
         x_rows = xT.rearrange("(p i) t -> p i t", i=PACK)
-        seed_rows = wgt.rearrange("(h r) c -> h r c", r=LIST_ROWS)[:, 0, 0 : 2 * J].rearrange("h (s c) -> h s c", c=SEED)
+        seed_rows = wgt.rearrange("(h r) c -> h r c", r=LIST_ROWS)[:, 0, J : 2 * J].rearrange("h (s c) -> h s c", c=SEED)
         nc.sync.dma_start(out=seeds[:], in_=seed_rows)
         nc.sync.dma_start(out=raw_words[:].bitcast(I32), in_=w_words[0].bitcast(I32))
         nc.sync.dma_start(out=planes[0][:], in_=x_rows[:, 0, :])
         nc.sync.dma_start(out=offsets[:], in_=offs)
+        nc.sync.dma_start(out=weights[:, 0:J], in_=wgt[:, 0:J])
         nc.sync.dma_start(out=planes[1][:], in_=x_rows[:, 1, :])
         for q in range(4):
             nc.sync.dma_start(out=raw_scales[32 * q : 32 * q + 4, :].bitcast(I32), in_=w_scales[0, 4 * q : 4 * q + 4, :].bitcast(I32))
         for i in range(2, PACK):
             nc.sync.dma_start(out=planes[i][:], in_=x_rows[:, i, :])
-        nc.sync.dma_start(out=weights[2][:], in_=wgt[:, 2 * J :])
+        nc.sync.dma_start(out=weights[:, 2 * J :], in_=wgt[:, 2 * J :])
         nc.sync.dma_start(out=bias[:], in_=b.rearrange("(p t) -> p t", t=PACK))
         nc.scalar.activation(out=warm2[:], in_=warm[:], func=GELU)
 
-        for blk in range(SEED // 32):
-            nc.vector.transpose(turned[:, 32 * blk : 32 * blk + 32], seeds[:, 32 * blk : 32 * blk + 32])
-        by_seed = turned[:].rearrange("p (g s) -> p s g", s=LIST_ROWS)
-        for c in range(2):
-            src = by_seed[:, 8 * c : 8 * c + 8, :].unsqueeze(3).to_broadcast([P, 8, 4, LIST_ROWS])
-            dst = spread[c][:].rearrange("p (s g r) -> p s g r", g=4, r=LIST_ROWS)
-            if c == 0:
-                nc.vector.tensor_copy(out=dst, in_=src)
-            else:
-                nc.scalar.copy(out=dst, in_=src)
-
+        nc.vector.transpose(turned[:], seeds[:])
         w_codes = keep.tile([P, 2 * N], U8, name="w_codes", align_bytes=64)
         w_plane = keep.tile([P, N], U8, name="w_plane", align_bytes=64)
-        for c in range(2):
-            nc.vector.transpose(weights[c][:], spread[c][:])
+        nc.vector.tensor_copy(
+            out=spread[:].rearrange("p (s g r) -> p s g r", g=2, r=LIST_ROWS),
+            in_=turned[:].rearrange("p (g s) -> p s g", s=LIST_ROWS).unsqueeze(3).to_broadcast([P, LIST_ROWS, 2, LIST_ROWS]),
+        )
         nc.vector.tensor_copy(
             out=w_codes[:].bitcast(U16).rearrange("p (t m) -> p t m", t=PACK),
             in_=raw_words[:].bitcast(U16).rearrange("p (m t) -> p t m", t=PACK),
         )
+        nc.vector.transpose(weights[:, J : 2 * J], spread[:])
 
         def gather(dst, i, c, j0, width):
             first = c * J + j0
             picks = offsets[:, first // LIST_ROWS : (first + width) // LIST_ROWS]
-            nc.vector.tensor_tensor(dst, planes[i][:].indirect(picks), weights[c][:, j0 : j0 + width], MULT)
+            nc.vector.tensor_tensor(dst, planes[i][:].indirect(picks), weights[:, first : first + width], MULT)
 
         def quantize(rounded, width, name):
             codes = keep.tile([P, width], U32, name="codes" + name, tag="codes" + name, align_bytes=64)
@@ -107,7 +101,7 @@ def tile_list_max_geluP_kernel(tc, xT, wgt, w_words, w_scales, b, offs, out_0, o
                 )
             return bank
 
-        picked = [keep.tile([P, PACK, J], F32, name="picked%d" % c) for c in range(2)]
+        picked = keep.tile([P, PACK, 2 * J], F32, name="picked")
         operands = {}
         first = {}
         of_two = {}
@@ -125,13 +119,16 @@ def tile_list_max_geluP_kernel(tc, xT, wgt, w_words, w_scales, b, offs, out_0, o
 
         def max_of_two(k):
             second = project(operands[1, k // 2], (k % 2) * PIECE)
-            of_two[k] = keep.tile([P, PACK, PIECE], F32, name="of_two%d" % k)
-            nc.vector.tensor_tensor(of_two[k][:], second[:], first[k][:], MAX)
+            if k < 2:
+                of_two[k] = keep.tile([P, PACK, PIECE], F32, name="of_two%d" % k)[:]
+            else:
+                of_two[k] = picked[:, :, J + (k - 2) * PIECE : J + (k - 1) * PIECE]
+            nc.vector.tensor_tensor(of_two[k], second[:], first[k][:], MAX)
 
         def max_of_three(k):
             third = project(operands[2, k // 2], (k % 2) * PIECE)
             of_three[k] = keep.tile([P, PACK, PIECE], F32, name="of_three%d" % k)
-            nc.vector.tensor_tensor(of_three[k][:], third[:], of_two[k][:], MAX)
+            nc.vector.tensor_tensor(of_three[k][:], third[:], of_two[k], MAX)
 
         y_plane = keep.tile([P, J], U8, name="y_plane", align_bytes=64)
         out_rows = out_0.rearrange("(p t) j -> p t j", t=PACK)
@@ -155,29 +152,28 @@ def tile_list_max_geluP_kernel(tc, xT, wgt, w_words, w_scales, b, offs, out_0, o
             nc.sync.dma_start(out=out_words[:, j0 : j0 + PIECE], in_=y_codes[:].bitcast(I32))
 
         for i in range(3):
-            for c in range(2):
-                gather(picked[c][:, i, :], i, c, 0, J)
+            gather(picked[:, i, :], i, 0, 0, 2 * J)
         nc.vector.tensor_copy(
             out=w_plane[:].rearrange("p (t m) -> p t m", t=PACK),
             in_=raw_scales[:].rearrange("p (m t) -> p t m", t=PACK),
         )
+        for h in range(2):
+            gather(picked[:, 3, h * HALF : (h + 1) * HALF], 3, 0, h * HALF, HALF)
+        gather(picked[:, 3, J:], 3, 1, 0, J)
         for c in range(2):
             for h in range(2):
-                gather(picked[c][:, 3, h * HALF : (h + 1) * HALF], 3, c, h * HALF, HALF)
-        for c in range(2):
-            for h in range(2):
-                round_unit(c, h, picked[c][:, :, h * HALF : (h + 1) * HALF])
+                round_unit(c, h, picked[:, :, c * J + h * HALF : c * J + (h + 1) * HALF])
         for h in range(2):
             for i in range(PACK):
-                gather(picked[h][:, i, 0:HALF], i, 2, h * HALF, HALF)
-        round_unit(2, 0, picked[0][:, :, 0:HALF])
+                gather(picked[:, i, h * J : h * J + HALF], i, 2, h * HALF, HALF)
+        round_unit(2, 0, picked[:, :, 0:HALF])
         for k in range(4):
             hold_first(k)
         for k in (0, 1):
             max_of_two(k)
         for k in (0, 1):
             max_of_three(k)
-        round_unit(2, 1, picked[1][:, :, 0:HALF])
+        round_unit(2, 1, picked[:, :, J : J + HALF])
         for k in (2, 3):
             max_of_two(k)
         for k in (0, 1):

@@ -23,7 +23,7 @@ PACK = 4
 PIECE = 128
 HALF = 256
 LIST_ROWS = 16
-SEED = 32
+SEED = 64
 
 
 def tile_list_max_geluP_kernel(tc, xT, wgt, w_words, w_scales, b, offs, out_0, out_1, out_2):
@@ -37,7 +37,7 @@ def tile_list_max_geluP_kernel(tc, xT, wgt, w_words, w_scales, b, offs, out_0, o
         weights = keep.tile([P, PICKS * J], F32, name="weights", align_bytes=64)
         seeds = keep.tile([P, SEED], F32, name="seeds", align_bytes=64)
         turned = keep.tile([P, SEED], F32, name="turned", align_bytes=64)
-        spread = keep.tile([P, J], F32, name="spread", align_bytes=64)
+        spread = keep.tile([P, 3 * HALF], F32, name="spread", align_bytes=64)
         raw_words = keep.tile([P, 2 * N], U8, name="raw_words")
         raw_scales = keep.tile([P, N], U8, name="raw_scales")
         bias = keep.tile([P, PACK], F32, name="bias")
@@ -47,33 +47,36 @@ def tile_list_max_geluP_kernel(tc, xT, wgt, w_words, w_scales, b, offs, out_0, o
         nc.vector.memset(warm[:], 0.0)
         nc.vector.memset(raw_scales[:].bitcast(I32), 0)
         x_rows = xT.rearrange("(p i) t -> p i t", i=PACK)
-        seed_rows = wgt.rearrange("(h r) c -> h r c", r=LIST_ROWS)[:, 0, J : 2 * J].rearrange("h (s c) -> h s c", c=SEED)
+        seed_rows = wgt.rearrange("(h r) c -> h r c", r=LIST_ROWS)[:, 0, 0 : 2 * J].rearrange("h (s c) -> h s c", c=SEED)
         nc.sync.dma_start(out=seeds[:], in_=seed_rows)
         nc.sync.dma_start(out=raw_words[:].bitcast(I32), in_=w_words[0].bitcast(I32))
         nc.sync.dma_start(out=planes[0][:], in_=x_rows[:, 0, :])
         nc.sync.dma_start(out=offsets[:], in_=offs)
-        nc.sync.dma_start(out=weights[:, 0:J], in_=wgt[:, 0:J])
+        nc.sync.dma_start(out=weights[:, 0:HALF], in_=wgt[:, 0:HALF])
         nc.sync.dma_start(out=planes[1][:], in_=x_rows[:, 1, :])
-        for q in range(4):
+        nc.sync.dma_start(out=planes[2][:], in_=x_rows[:, 2, :])
+        for q in range(3):
             nc.sync.dma_start(out=raw_scales[32 * q : 32 * q + 4, :].bitcast(I32), in_=w_scales[0, 4 * q : 4 * q + 4, :].bitcast(I32))
-        for i in range(2, PACK):
-            nc.sync.dma_start(out=planes[i][:], in_=x_rows[:, i, :])
+        nc.sync.dma_start(out=planes[3][:], in_=x_rows[:, 3, :])
+        for q in range(3, 4):
+            nc.sync.dma_start(out=raw_scales[32 * q : 32 * q + 4, :].bitcast(I32), in_=w_scales[0, 4 * q : 4 * q + 4, :].bitcast(I32))
         nc.sync.dma_start(out=weights[:, 2 * J :], in_=wgt[:, 2 * J :])
         nc.sync.dma_start(out=bias[:], in_=b.rearrange("(p t) -> p t", t=PACK))
         nc.scalar.activation(out=warm2[:], in_=warm[:], func=GELU)
 
-        nc.vector.transpose(turned[:], seeds[:])
+        for blk in range(2):
+            nc.vector.transpose(turned[:, 32 * blk : 32 * blk + 32], seeds[:, 32 * blk : 32 * blk + 32])
         w_codes = keep.tile([P, 2 * N], U8, name="w_codes", align_bytes=64)
         w_plane = keep.tile([P, N], U8, name="w_plane", align_bytes=64)
         nc.vector.tensor_copy(
-            out=spread[:].rearrange("p (s g r) -> p s g r", g=2, r=LIST_ROWS),
-            in_=turned[:].rearrange("p (g s) -> p s g", s=LIST_ROWS).unsqueeze(3).to_broadcast([P, LIST_ROWS, 2, LIST_ROWS]),
+            out=spread[:].rearrange("p (s g r) -> p s g r", g=4, r=LIST_ROWS),
+            in_=turned[:].rearrange("p (g s) -> p s g", s=LIST_ROWS)[:, 4:, :].unsqueeze(3).to_broadcast([P, 12, 4, LIST_ROWS]),
         )
         nc.vector.tensor_copy(
             out=w_codes[:].bitcast(U16).rearrange("p (t m) -> p t m", t=PACK),
             in_=raw_words[:].bitcast(U16).rearrange("p (m t) -> p t m", t=PACK),
         )
-        nc.vector.transpose(weights[:, J : 2 * J], spread[:])
+        nc.vector.transpose(weights[:, HALF : 2 * J], spread[:])
 
         def gather(dst, i, c, j0, width):
             first = c * J + j0
@@ -101,15 +104,19 @@ def tile_list_max_geluP_kernel(tc, xT, wgt, w_words, w_scales, b, offs, out_0, o
                 )
             return bank
 
-        picked = keep.tile([P, PACK, 2 * J], F32, name="picked")
+        picked = [keep.tile([P, PACK, J], F32, name="picked%d" % c) for c in range(2)]
         operands = {}
         first = {}
         of_two = {}
         of_three = {}
 
-        def round_unit(c, h, rows):
+        def round_unit(c, h, rows, step=HALF):
             rounded = keep.tile([P, HALF, PACK], BF16, name="rounded%d_%d" % (c, h), align_bytes=64)
-            nc.scalar.copy(out=rounded[:].rearrange("p (a e) i -> p a i e", e=4), in_=rows.rearrange("p i (a e) -> p a i e", e=4))
+            for j0 in range(0, HALF, step):
+                nc.scalar.copy(
+                    out=rounded[:, j0 : j0 + step, :].rearrange("p (a e) i -> p a i e", e=4),
+                    in_=rows[:, :, j0 : j0 + step].rearrange("p i (a e) -> p a i e", e=4),
+                )
             operands[c, h] = quantize(rounded, HALF, "%d_%d" % (c, h))
 
         def hold_first(k):
@@ -122,7 +129,7 @@ def tile_list_max_geluP_kernel(tc, xT, wgt, w_words, w_scales, b, offs, out_0, o
             if k < 2:
                 of_two[k] = keep.tile([P, PACK, PIECE], F32, name="of_two%d" % k)[:]
             else:
-                of_two[k] = picked[:, :, J + (k - 2) * PIECE : J + (k - 1) * PIECE]
+                of_two[k] = picked[1][:, k - 2, :].rearrange("p (t j) -> p t j", t=PACK)
             nc.vector.tensor_tensor(of_two[k], second[:], first[k][:], MAX)
 
         def max_of_three(k):
@@ -134,54 +141,61 @@ def tile_list_max_geluP_kernel(tc, xT, wgt, w_words, w_scales, b, offs, out_0, o
         out_rows = out_0.rearrange("(p t) j -> p t j", t=PACK)
         out_words = out_1[0].rearrange("p j i -> p (j i)").bitcast(I32)
 
+        y_rounded = [keep.tile([P, HALF, PACK], BF16, name="y_rounded%d" % h, align_bytes=64) for h in range(2)]
+
         def finish(k):
             j0 = k * PIECE
             y = keep.tile([P, PACK, PIECE], F32, name="y%d" % k)
             for t in range(PACK):
                 nc.scalar.activation(out=y[:, t, :], in_=of_three[k][:, t, :], func=GELU, bias=bias[:, t : t + 1])
             nc.sync.dma_start(out=out_rows[:, :, j0 : j0 + PIECE], in_=y[:])
-            y_rounded = keep.tile([P, PIECE, PACK], BF16, name="y_rounded%d" % k, align_bytes=64)
-            dst = y_rounded[:].rearrange("p (a e) t -> p a t e", e=4)
+            dst = y_rounded[k // 2][:, j0 % HALF : j0 % HALF + PIECE, :].rearrange("p (a e) t -> p a t e", e=4)
             src = y[:].rearrange("p t (a e) -> p a t e", e=4)
             if k >= 2:
                 nc.vector.tensor_copy(out=dst, in_=src)
             else:
                 nc.scalar.copy(out=dst, in_=src)
-            y_codes = keep.tile([P, PIECE], U32, name="y_codes%d" % k, align_bytes=64)
-            nc.vector.quantize_mx(out=y_codes[:].bitcast(FP8X4), scales=y_plane[:, j0 : j0 + PIECE], in_=y_rounded[:].rearrange("p j t -> p (j t)"))
-            nc.sync.dma_start(out=out_words[:, j0 : j0 + PIECE], in_=y_codes[:].bitcast(I32))
+
+        def hand_on(h):
+            j0 = h * HALF
+            y_codes = keep.tile([P, HALF], U32, name="y_codes%d" % h, align_bytes=64)
+            nc.vector.quantize_mx(out=y_codes[:].bitcast(FP8X4), scales=y_plane[:, j0 : j0 + HALF], in_=y_rounded[h][:].rearrange("p j t -> p (j t)"))
+            nc.sync.dma_start(out=out_words[:, j0 : j0 + HALF], in_=y_codes[:].bitcast(I32))
 
         for i in range(3):
-            gather(picked[:, i, :], i, 0, 0, 2 * J)
+            for c in range(2):
+                gather(picked[c][:, i, :], i, c, 0, J)
+        for j0, width in ((0, PIECE), (PIECE, PIECE), (HALF, HALF)):
+            gather(picked[0][:, 3, j0 : j0 + width], 3, 0, j0, width)
+        gather(picked[1][:, 3, :], 3, 1, 0, J)
         nc.vector.tensor_copy(
             out=w_plane[:].rearrange("p (t m) -> p t m", t=PACK),
             in_=raw_scales[:].rearrange("p (m t) -> p t m", t=PACK),
         )
-        for h in range(2):
-            gather(picked[:, 3, h * HALF : (h + 1) * HALF], 3, 0, h * HALF, HALF)
-        gather(picked[:, 3, J:], 3, 1, 0, J)
         for c in range(2):
             for h in range(2):
-                round_unit(c, h, picked[:, :, c * J + h * HALF : c * J + (h + 1) * HALF])
+                round_unit(c, h, picked[c][:, :, h * HALF : (h + 1) * HALF], PIECE if (c, h) == (0, 0) else HALF)
         for h in range(2):
             for i in range(PACK):
-                gather(picked[:, i, h * J : h * J + HALF], i, 2, h * HALF, HALF)
-        round_unit(2, 0, picked[:, :, 0:HALF])
+                gather(picked[h][:, i, 0:HALF], i, 2, h * HALF, HALF)
+        round_unit(2, 0, picked[0][:, :, 0:HALF])
         for k in range(4):
             hold_first(k)
         for k in (0, 1):
             max_of_two(k)
         for k in (0, 1):
             max_of_three(k)
-        round_unit(2, 1, picked[:, :, J : J + HALF])
+        round_unit(2, 1, picked[1][:, :, 0:HALF])
         for k in (2, 3):
             max_of_two(k)
         for k in (0, 1):
             finish(k)
         for k in (2, 3):
             max_of_three(k)
+        hand_on(0)
         for k in (2, 3):
             finish(k)
+        hand_on(1)
         for q in range(4):
             queue = nc.scalar if q % 2 else nc.sync
             queue.dma_start(out=out_2[0, 4 * q : 4 * q + 4, :].bitcast(I32), in_=y_plane[32 * q : 32 * q + 4, :].bitcast(I32))

@@ -114,8 +114,8 @@ def tile_list_max_geluP_kernel(tc, xT, wgt, w_words, w_scales, b, offs, out_0, o
             rounded = keep.tile([P, HALF, PACK], BF16, name="rounded%d_%d" % (c, h), align_bytes=64)
             for j0 in range(0, HALF, step):
                 nc.scalar.copy(
-                    out=rounded[:, j0 : j0 + step, :].rearrange("p (a e) i -> p a i e", e=4),
-                    in_=rows[:, :, j0 : j0 + step].rearrange("p i (a e) -> p a i e", e=4),
+                    out=rounded[:, j0 : j0 + step, :].rearrange("p (a e) i -> p a i e", e=2),
+                    in_=rows[:, :, j0 : j0 + step].rearrange("p i (a e) -> p a i e", e=2),
                 )
             operands[c, h] = quantize(rounded, HALF, "%d_%d" % (c, h))
 
@@ -149,12 +149,14 @@ def tile_list_max_geluP_kernel(tc, xT, wgt, w_words, w_scales, b, offs, out_0, o
             for t in range(PACK):
                 nc.scalar.activation(out=y[:, t, :], in_=of_three[k][:, t, :], func=GELU, bias=bias[:, t : t + 1])
             nc.sync.dma_start(out=out_rows[:, :, j0 : j0 + PIECE], in_=y[:])
-            dst = y_rounded[k // 2][:, j0 % HALF : j0 % HALF + PIECE, :].rearrange("p (a e) t -> p a t e", e=4)
-            src = y[:].rearrange("p t (a e) -> p a t e", e=4)
-            if k >= 2:
-                nc.vector.tensor_copy(out=dst, in_=src)
-            else:
-                nc.scalar.copy(out=dst, in_=src)
+            return y
+
+        def round_y(copy, y, k, lo, hi):
+            at = (k % 2) * PIECE
+            copy(
+                out=y_rounded[k // 2][:, at + lo : at + hi, :].rearrange("p (a e) t -> p a t e", e=4),
+                in_=y[:, :, lo:hi].rearrange("p t (a e) -> p a t e", e=4),
+            )
 
         def hand_on(h):
             j0 = h * HALF
@@ -188,13 +190,18 @@ def tile_list_max_geluP_kernel(tc, xT, wgt, w_words, w_scales, b, offs, out_0, o
         round_unit(2, 1, picked[1][:, :, 0:HALF])
         for k in (2, 3):
             max_of_two(k)
-        for k in (0, 1):
-            finish(k)
+        ys = {0: finish(0)}
+        round_y(nc.scalar.copy, ys[0], 0, 0, PIECE)
+        ys[1] = finish(1)
         for k in (2, 3):
             max_of_three(k)
-        hand_on(0)
+        round_y(nc.vector.tensor_copy, ys[1], 1, 0, PIECE)
         for k in (2, 3):
-            finish(k)
+            ys[k] = finish(k)
+        round_y(nc.vector.tensor_copy, ys[2], 2, 0, PIECE)
+        hand_on(0)
+        round_y(nc.scalar.copy, ys[3], 3, 0, PIECE // 2)
+        round_y(nc.vector.tensor_copy, ys[3], 3, PIECE // 2, PIECE)
         hand_on(1)
         for q in range(4):
             queue = nc.scalar if q % 2 else nc.sync

@@ -54,12 +54,10 @@ def tile_list_max_geluP_kernel(tc, xT, wgt, w_words, w_scales, b, offs, out_0, o
         nc.sync.dma_start(out=offsets[:], in_=offs)
         nc.sync.dma_start(out=weights[:, 0:HALF], in_=wgt[:, 0:HALF])
         nc.sync.dma_start(out=planes[1][:], in_=x_rows[:, 1, :])
+        for q in range(4):
+            nc.sync.dma_start(out=raw_scales[32 * q : 32 * q + 4, :].bitcast(I32), in_=w_scales[0, 4 * q : 4 * q + 4, :].bitcast(I32))
         nc.sync.dma_start(out=planes[2][:], in_=x_rows[:, 2, :])
-        for q in range(3):
-            nc.sync.dma_start(out=raw_scales[32 * q : 32 * q + 4, :].bitcast(I32), in_=w_scales[0, 4 * q : 4 * q + 4, :].bitcast(I32))
         nc.sync.dma_start(out=planes[3][:], in_=x_rows[:, 3, :])
-        for q in range(3, 4):
-            nc.sync.dma_start(out=raw_scales[32 * q : 32 * q + 4, :].bitcast(I32), in_=w_scales[0, 4 * q : 4 * q + 4, :].bitcast(I32))
         nc.sync.dma_start(out=weights[:, 2 * J :], in_=wgt[:, 2 * J :])
         nc.sync.dma_start(out=bias[:], in_=b.rearrange("(p t) -> p t", t=PACK))
         nc.scalar.activation(out=warm2[:], in_=warm[:], func=GELU)
@@ -86,7 +84,7 @@ def tile_list_max_geluP_kernel(tc, xT, wgt, w_words, w_scales, b, offs, out_0, o
         def quantize(rounded, width, name):
             codes = keep.tile([P, width], U32, name="codes" + name, tag="codes" + name, align_bytes=64)
             scales = keep.tile([P, width], U8, name="scales" + name, align_bytes=64)
-            nc.vector.quantize_mx(out=codes[:].bitcast(FP8X4), scales=scales[:], in_=rounded[:].rearrange("p j i -> p (j i)"))
+            nc.vector.quantize_mx(out=codes[:].bitcast(FP8X4), scales=scales[:], in_=rounded.rearrange("p j i -> p (j i)"))
             return codes, scales
 
         def project(operand, at):
@@ -104,32 +102,33 @@ def tile_list_max_geluP_kernel(tc, xT, wgt, w_words, w_scales, b, offs, out_0, o
                 )
             return bank
 
-        picked = [keep.tile([P, PACK, J], F32, name="picked%d" % c) for c in range(2)]
+        rows = keep.tile([P, 2 + 4 * PACK, HALF], F32, name="rows")
+        picked = rows[:, 2:, :].rearrange("p (i u) j -> p i (u j)", i=PACK)
         operands = {}
         first = {}
         of_two = {}
         of_three = {}
 
-        def round_unit(c, h, rows, step=HALF):
-            rounded = keep.tile([P, HALF, PACK], BF16, name="rounded%d_%d" % (c, h), align_bytes=64)
-            for j0 in range(0, HALF, step):
-                nc.scalar.copy(
-                    out=rounded[:, j0 : j0 + step, :].rearrange("p (a e) i -> p a i e", e=2),
-                    in_=rows[:, :, j0 : j0 + step].rearrange("p i (a e) -> p a i e", e=2),
-                )
-            operands[c, h] = quantize(rounded, HALF, "%d_%d" % (c, h))
+        rounded = [keep.tile([P, J, PACK], BF16, name="rounded%d" % c, align_bytes=64) for c in range(PICKS)]
+
+        def round_rows(c, j0, src):
+            width = src.shape[2]
+            nc.scalar.copy(
+                out=rounded[c][:, j0 : j0 + width, :].rearrange("p (a e) i -> p a i e", e=2),
+                in_=src.rearrange("p i (a e) -> p a i e", e=2),
+            )
 
         def hold_first(k):
-            bank = project(operands[0, k // 2], (k % 2) * PIECE)
+            bank = project(operands[0], k * PIECE)
             first[k] = keep.tile([P, PACK, PIECE], F32, name="first%d" % k)
             nc.scalar.copy(out=first[k][:], in_=bank[:])
 
         def max_of_two(k):
-            second = project(operands[1, k // 2], (k % 2) * PIECE)
+            second = project(operands[1], k * PIECE)
             if k < 2:
                 of_two[k] = keep.tile([P, PACK, PIECE], F32, name="of_two%d" % k)[:]
             else:
-                of_two[k] = picked[1][:, k - 2, :].rearrange("p (t j) -> p t j", t=PACK)
+                of_two[k] = rows[:, 2 * k : 2 * k + 2, :].rearrange("p r (t j) -> p (r t) j", t=2)
             nc.vector.tensor_tensor(of_two[k], second[:], first[k][:], MAX)
 
         def max_of_three(k):
@@ -165,29 +164,32 @@ def tile_list_max_geluP_kernel(tc, xT, wgt, w_words, w_scales, b, offs, out_0, o
             nc.sync.dma_start(out=out_words[:, j0 : j0 + HALF], in_=y_codes[:].bitcast(I32))
 
         for i in range(3):
-            for c in range(2):
-                gather(picked[c][:, i, :], i, c, 0, J)
-        for j0, width in ((0, PIECE), (PIECE, PIECE), (HALF, HALF)):
-            gather(picked[0][:, 3, j0 : j0 + width], 3, 0, j0, width)
-        gather(picked[1][:, 3, :], 3, 1, 0, J)
+            gather(picked[:, i, :], i, 0, 0, 2 * J)
         nc.vector.tensor_copy(
             out=w_plane[:].rearrange("p (t m) -> p t m", t=PACK),
             in_=raw_scales[:].rearrange("p (m t) -> p t m", t=PACK),
         )
-        for c in range(2):
-            for h in range(2):
-                round_unit(c, h, picked[c][:, :, h * HALF : (h + 1) * HALF], PIECE if (c, h) == (0, 0) else HALF)
+        for j0, j1 in ((0, PIECE), (PIECE, J), (J, 2 * J)):
+            gather(picked[:, 3, j0:j1], 3, 0, j0, j1 - j0)
+        for j0, j1 in ((0, PIECE), (PIECE, HALF), (HALF, J)):
+            round_rows(0, j0, picked[:, :, j0:j1])
+        operands[0] = quantize(rounded[0][:], J, "0")
+        for j0 in (0, HALF):
+            round_rows(1, j0, picked[:, :, J + j0 : J + j0 + HALF])
+        operands[1] = quantize(rounded[1][:], J, "1")
         for h in range(2):
             for i in range(PACK):
-                gather(picked[h][:, i, 0:HALF], i, 2, h * HALF, HALF)
-        round_unit(2, 0, picked[0][:, :, 0:HALF])
+                gather(rows[:, PACK * h + i, :], i, 2, h * HALF, HALF)
+        round_rows(2, 0, rows[:, 0:PACK, :])
+        operands[2, 0] = quantize(rounded[2][:, 0:HALF, :], HALF, "2_0")
         for k in range(4):
             hold_first(k)
         for k in (0, 1):
             max_of_two(k)
         for k in (0, 1):
             max_of_three(k)
-        round_unit(2, 1, picked[1][:, :, 0:HALF])
+        round_rows(2, HALF, rows[:, PACK : 2 * PACK, :])
+        operands[2, 1] = quantize(rounded[2][:, HALF:, :], HALF, "2_1")
         for k in (2, 3):
             max_of_two(k)
         ys = {0: finish(0)}

@@ -123,18 +123,25 @@ def tile_list_max_geluP_kernel(tc, xT, wgt, w_words, w_scales, b, offs, out_0, o
             first[k] = keep.tile([P, PACK, PIECE], F32, name="first%d" % k)
             nc.scalar.copy(out=first[k][:], in_=bank[:])
 
+        def two_rows(r):
+            return rows[:, r : r + 2, :].rearrange("p r (t j) -> p (r t) j", t=2)
+
         def max_of_two(k):
             second = project(operands[1], k * PIECE)
             if k < 2:
                 of_two[k] = keep.tile([P, PACK, PIECE], F32, name="of_two%d" % k)[:]
             else:
-                of_two[k] = rows[:, 2 * k : 2 * k + 2, :].rearrange("p r (t j) -> p (r t) j", t=2)
+                of_two[k] = two_rows(2 * k + 1)
             nc.vector.tensor_tensor(of_two[k], second[:], first[k][:], MAX)
 
         def max_of_three(k):
             third = project(operands[2, k // 2], (k % 2) * PIECE)
-            of_three[k] = keep.tile([P, PACK, PIECE], F32, name="of_three%d" % k)
-            nc.vector.tensor_tensor(of_three[k][:], third[:], of_two[k], MAX)
+            if k == 1:
+                of_three[k] = two_rows(3)
+            else:
+                of_three[k] = keep.tile([P, PACK, PIECE], F32, name="of_three%d" % k)[:]
+            for t0, t1 in ((0, 2), (2, 4)) if k == 3 else ((0, 4),):
+                nc.vector.tensor_tensor(of_three[k][:, t0:t1, :], third[:, t0:t1, :], of_two[k][:, t0:t1, :], MAX)
 
         y_plane = keep.tile([P, J], U8, name="y_plane", align_bytes=64)
         out_rows = out_0.rearrange("(p t) j -> p t j", t=PACK)
@@ -157,11 +164,17 @@ def tile_list_max_geluP_kernel(tc, xT, wgt, w_words, w_scales, b, offs, out_0, o
                 in_=y[:, :, lo:hi].rearrange("p t (a e) -> p a t e", e=4),
             )
 
-        def hand_on(h):
-            j0 = h * HALF
-            y_codes = keep.tile([P, HALF], U32, name="y_codes%d" % h, align_bytes=64)
-            nc.vector.quantize_mx(out=y_codes[:].bitcast(FP8X4), scales=y_plane[:, j0 : j0 + HALF], in_=y_rounded[h][:].rearrange("p j t -> p (j t)"))
-            nc.sync.dma_start(out=out_words[:, j0 : j0 + HALF], in_=y_codes[:].bitcast(I32))
+        y_codes = [keep.tile([P, HALF], U32, name="y_codes%d" % h, align_bytes=64) for h in range(2)]
+
+        def hand_on(j0, width):
+            at = j0 % HALF
+            nc.vector.quantize_mx(
+                out=y_codes[j0 // HALF][:, at : at + width].bitcast(FP8X4),
+                scales=y_plane[:, j0 : j0 + width],
+                in_=y_rounded[j0 // HALF][:, at : at + width, :].rearrange("p j t -> p (j t)"),
+            )
+            if at + width == HALF:
+                nc.sync.dma_start(out=out_words[:, j0 - at : j0 - at + HALF], in_=y_codes[j0 // HALF][:].bitcast(I32))
 
         for i in range(3):
             gather(picked[:, i, :], i, 0, 0, 2 * J)
@@ -182,29 +195,30 @@ def tile_list_max_geluP_kernel(tc, xT, wgt, w_words, w_scales, b, offs, out_0, o
                 gather(rows[:, PACK * h + i, :], i, 2, h * HALF, HALF)
         round_rows(2, 0, rows[:, 0:PACK, :])
         operands[2, 0] = quantize(rounded[2][:, 0:HALF, :], HALF, "2_0")
-        for k in range(4):
+        for k in range(3):
             hold_first(k)
         for k in (0, 1):
             max_of_two(k)
-        for k in (0, 1):
-            max_of_three(k)
+        max_of_three(0)
         round_rows(2, HALF, rows[:, PACK : 2 * PACK, :])
+        hold_first(3)
         operands[2, 1] = quantize(rounded[2][:, HALF:, :], HALF, "2_1")
-        for k in (2, 3):
-            max_of_two(k)
+        max_of_three(1)
+        max_of_two(2)
+        max_of_three(2)
+        max_of_two(3)
+        max_of_three(3)
         ys = {0: finish(0)}
         round_y(nc.scalar.copy, ys[0], 0, 0, PIECE)
-        ys[1] = finish(1)
-        for k in (2, 3):
-            max_of_three(k)
-        round_y(nc.vector.tensor_copy, ys[1], 1, 0, PIECE)
-        for k in (2, 3):
+        for k in (1, 2, 3):
             ys[k] = finish(k)
+        round_y(nc.vector.tensor_copy, ys[1], 1, 0, PIECE)
         round_y(nc.vector.tensor_copy, ys[2], 2, 0, PIECE)
-        hand_on(0)
+        hand_on(0, HALF)
+        hand_on(HALF, PIECE)
         round_y(nc.scalar.copy, ys[3], 3, 0, PIECE // 2)
         round_y(nc.vector.tensor_copy, ys[3], 3, PIECE // 2, PIECE)
-        hand_on(1)
+        hand_on(HALF + PIECE, PIECE)
         for q in range(4):
             queue = nc.scalar if q % 2 else nc.sync
             queue.dma_start(out=out_2[0, 4 * q : 4 * q + 4, :].bitcast(I32), in_=y_plane[32 * q : 32 * q + 4, :].bitcast(I32))

@@ -16,6 +16,7 @@ FP8X4 = mybir.dt.float8_e4m3fn_x4
 FP4X4 = mybir.dt.float4_e2m1fn_x4
 MULT = mybir.AluOpType.mult
 MAX = mybir.AluOpType.max
+ADD = mybir.AluOpType.add
 GELU = mybir.ActivationFunctionType.Gelu_apprx_tanh
 
 P = 128
@@ -109,7 +110,7 @@ def tile_list_max_geluP_kernel(tc, xT, wgt, w_words, w_scales, b, offs, out_0, o
         of_two = {}
         of_three = {}
 
-        rounded = [keep.tile([P, J, PACK], BF16, name="rounded%d" % c, align_bytes=64) for c in range(PICKS)]
+        rounded = [keep.tile([P, J + PIECE, PACK], BF16, name="rounded%d" % c, align_bytes=64) for c in range(PICKS)]
 
         def round_rows(c, j0, src):
             width = src.shape[2]
@@ -123,21 +124,30 @@ def tile_list_max_geluP_kernel(tc, xT, wgt, w_words, w_scales, b, offs, out_0, o
             first[k] = keep.tile([P, PACK, PIECE], F32, name="first%d" % k)
             nc.scalar.copy(out=first[k][:], in_=bank[:])
 
-        def two_rows(r):
-            return rows[:, r : r + 2, :].rearrange("p r (t j) -> p (r t) j", t=2)
+        flat = rows[:].rearrange("p r j -> p (r j)")
+        late = PACK * HALF + PIECE
+
+        def freed(at):
+            return flat[:, at : at + J].rearrange("p (t j) -> p t j", t=PACK)
+
+        seconds = {}
+
+        def part_of_two(k, t0, t1):
+            nc.vector.tensor_tensor(of_two[k][:, t0:t1, :], seconds[k][:, t0:t1, :], first[k][:, t0:t1, :], MAX)
 
         def max_of_two(k):
             second = project(operands[1], k * PIECE)
-            if k < 2:
-                of_two[k] = keep.tile([P, PACK, PIECE], F32, name="of_two%d" % k)[:]
+            if k == 2:
+                of_two[k] = freed(late)
             else:
-                of_two[k] = two_rows(2 * k + 1)
-            nc.vector.tensor_tensor(of_two[k], second[:], first[k][:], MAX)
+                of_two[k] = keep.tile([P, PACK, PIECE], F32, name="of_two%d" % k)[:]
+            seconds[k] = second
+            part_of_two(k, 0, 2 if k == 3 else PACK)
 
         def max_of_three(k):
-            third = project(operands[2, k // 2], (k % 2) * PIECE)
+            third = project(operands[2, max(k, 1)], PIECE if k == 1 else 0)
             if k == 1:
-                of_three[k] = two_rows(3)
+                of_three[k] = freed(late - J)
             else:
                 of_three[k] = keep.tile([P, PACK, PIECE], F32, name="of_three%d" % k)[:]
             for t0, t1 in ((0, 2), (2, 4)) if k == 3 else ((0, 4),):
@@ -147,7 +157,7 @@ def tile_list_max_geluP_kernel(tc, xT, wgt, w_words, w_scales, b, offs, out_0, o
         out_rows = out_0.rearrange("(p t) j -> p t j", t=PACK)
         out_words = out_1[0].rearrange("p j i -> p (j i)").bitcast(I32)
 
-        y_rounded = [keep.tile([P, HALF, PACK], BF16, name="y_rounded%d" % h, align_bytes=64) for h in range(2)]
+        y_rounded = [rounded[2][:, J - PIECE :, :], keep.tile([P, HALF, PACK], BF16, name="y_rounded1", align_bytes=64)[:]]
 
         def finish(k):
             j0 = k * PIECE
@@ -156,6 +166,11 @@ def tile_list_max_geluP_kernel(tc, xT, wgt, w_words, w_scales, b, offs, out_0, o
                 nc.scalar.activation(out=y[:, t, :], in_=of_three[k][:, t, :], func=GELU, bias=bias[:, t : t + 1])
             nc.sync.dma_start(out=out_rows[:, :, j0 : j0 + PIECE], in_=y[:])
             return y
+
+        def round_on_pool(y, k):
+            nc.gpsimd.tensor_scalar(
+                y_rounded[0][:, k * PIECE : (k + 1) * PIECE, :], y[:].rearrange("p t j -> p j t"), 1.0, 0.0, MULT, ADD
+            )
 
         def round_y(copy, y, k, lo, hi):
             at = (k % 2) * PIECE
@@ -186,33 +201,37 @@ def tile_list_max_geluP_kernel(tc, xT, wgt, w_words, w_scales, b, offs, out_0, o
             gather(picked[:, 3, j0:j1], 3, 0, j0, j1 - j0)
         for j0, j1 in ((0, PIECE), (PIECE, HALF), (HALF, J)):
             round_rows(0, j0, picked[:, :, j0:j1])
-        operands[0] = quantize(rounded[0][:], J, "0")
+        operands[0] = quantize(rounded[0][:, 0:J, :], J, "0")
         for j0 in (0, HALF):
             round_rows(1, j0, picked[:, :, J + j0 : J + j0 + HALF])
-        operands[1] = quantize(rounded[1][:], J, "1")
+        operands[1] = quantize(rounded[1][:, 0:J, :], J, "1")
         for h in range(2):
             for i in range(PACK):
                 gather(rows[:, PACK * h + i, :], i, 2, h * HALF, HALF)
         round_rows(2, 0, rows[:, 0:PACK, :])
-        operands[2, 0] = quantize(rounded[2][:, 0:HALF, :], HALF, "2_0")
+        operands[2, 1] = quantize(rounded[2][:, 0:HALF, :], HALF, "2_1")
         for k in range(3):
             hold_first(k)
         for k in (0, 1):
             max_of_two(k)
         max_of_three(0)
-        round_rows(2, HALF, rows[:, PACK : 2 * PACK, :])
+        for k in (2, 3):
+            at = (k - 2) * PIECE
+            round_rows(2, k * PIECE, rows[:, PACK : 2 * PACK, at : at + PIECE])
         hold_first(3)
-        operands[2, 1] = quantize(rounded[2][:, HALF:, :], HALF, "2_1")
+        operands[2, 2] = quantize(rounded[2][:, 2 * PIECE : 3 * PIECE, :], PIECE, "2_2")
         max_of_three(1)
+        operands[2, 3] = quantize(rounded[2][:, 3 * PIECE : J, :], PIECE, "2_3")
         max_of_two(2)
-        max_of_three(2)
         max_of_two(3)
+        max_of_three(2)
+        part_of_two(3, 2, PACK)
         max_of_three(3)
-        ys = {0: finish(0)}
-        round_y(nc.scalar.copy, ys[0], 0, 0, PIECE)
-        for k in (1, 2, 3):
+        ys = {k: finish(k) for k in (0, 1)}
+        for k in (0, 1):
+            round_on_pool(ys[k], k)
+        for k in (2, 3):
             ys[k] = finish(k)
-        round_y(nc.vector.tensor_copy, ys[1], 1, 0, PIECE)
         round_y(nc.vector.tensor_copy, ys[2], 2, 0, PIECE)
         hand_on(0, HALF)
         hand_on(HALF, PIECE)

@@ -1,6 +1,7 @@
 from contextlib import ExitStack
 
 import concourse.mybir as mybir
+from concourse.masks import make_identity
 
 K, N, T, J = 512, 512, 2048, 512
 PICKS = 3
@@ -24,7 +25,7 @@ PACK = 4
 PIECE = 128
 HALF = 256
 LIST_ROWS = 16
-SEED = 64
+SEED = 32
 
 
 def tile_list_max_geluP_kernel(tc, xT, wgt, w_words, w_scales, b, offs, out_0, out_1, out_2):
@@ -36,9 +37,10 @@ def tile_list_max_geluP_kernel(tc, xT, wgt, w_words, w_scales, b, offs, out_0, o
         offsets = keep.tile([P, PICKS * J // LIST_ROWS], U16, name="offsets")
         planes = [keep.tile([P, T], F32, name="plane%d" % i) for i in range(PACK)]
         weights = keep.tile([P, PICKS * J], F32, name="weights", align_bytes=64)
-        seeds = keep.tile([P, SEED], F32, name="seeds", align_bytes=64)
-        turned = keep.tile([P, SEED], F32, name="turned", align_bytes=64)
-        spread = keep.tile([P, 3 * HALF], F32, name="spread", align_bytes=64)
+        seeds = [keep.tile([P, SEED], F32, name="seeds%d" % c, align_bytes=64) for c in range(2)]
+        turned = [keep.tile([P, SEED], F32, name="turned%d" % c, align_bytes=64) for c in range(2)]
+        spread = [keep.tile([P, J], F32, name="spread%d" % c, align_bytes=64) for c in range(2)]
+        identity = keep.tile([P, P], F32, name="identity")
         raw_words = keep.tile([P, 2 * N], U8, name="raw_words")
         raw_scales = keep.tile([P, N], U8, name="raw_scales")
         bias = keep.tile([P, PACK], F32, name="bias")
@@ -48,12 +50,13 @@ def tile_list_max_geluP_kernel(tc, xT, wgt, w_words, w_scales, b, offs, out_0, o
         nc.vector.memset(warm[:], 0.0)
         nc.vector.memset(raw_scales[:].bitcast(I32), 0)
         x_rows = xT.rearrange("(p i) t -> p i t", i=PACK)
-        seed_rows = wgt.rearrange("(h r) c -> h r c", r=LIST_ROWS)[:, 0, 0 : 2 * J].rearrange("h (s c) -> h s c", c=SEED)
-        nc.sync.dma_start(out=seeds[:], in_=seed_rows)
+        make_identity(nc, identity[:])
+        head_rows = wgt.rearrange("(h r) c -> h r c", r=LIST_ROWS)[:, 0, :]
+        nc.sync.dma_start(out=seeds[0][:], in_=head_rows[:, 0:J].rearrange("h (s c) -> h s c", c=SEED))
+        nc.sync.dma_start(out=seeds[1][:], in_=head_rows[:, J : 2 * J].rearrange("h (u c) -> u h c", c=SEED))
         nc.sync.dma_start(out=raw_words[:].bitcast(I32), in_=w_words[0].bitcast(I32))
-        nc.sync.dma_start(out=planes[0][:], in_=x_rows[:, 0, :])
         nc.sync.dma_start(out=offsets[:], in_=offs)
-        nc.sync.dma_start(out=weights[:, 0:HALF], in_=wgt[:, 0:HALF])
+        nc.sync.dma_start(out=planes[0][:], in_=x_rows[:, 0, :])
         nc.sync.dma_start(out=planes[1][:], in_=x_rows[:, 1, :])
         for q in range(4):
             nc.sync.dma_start(out=raw_scales[32 * q : 32 * q + 4, :].bitcast(I32), in_=w_scales[0, 4 * q : 4 * q + 4, :].bitcast(I32))
@@ -63,19 +66,34 @@ def tile_list_max_geluP_kernel(tc, xT, wgt, w_words, w_scales, b, offs, out_0, o
         nc.sync.dma_start(out=bias[:], in_=b.rearrange("(p t) -> p t", t=PACK))
         nc.scalar.activation(out=warm2[:], in_=warm[:], func=GELU)
 
-        for blk in range(2):
-            nc.vector.transpose(turned[:, 32 * blk : 32 * blk + 32], seeds[:, 32 * blk : 32 * blk + 32])
+        for c in range(2):
+            nc.vector.transpose(turned[c][:], seeds[c][:])
         w_codes = keep.tile([P, 2 * N], U8, name="w_codes", align_bytes=64)
         w_plane = keep.tile([P, N], U8, name="w_plane", align_bytes=64)
         nc.vector.tensor_copy(
-            out=spread[:].rearrange("p (s g r) -> p s g r", g=4, r=LIST_ROWS),
-            in_=turned[:].rearrange("p (g s) -> p s g", s=LIST_ROWS)[:, 4:, :].unsqueeze(3).to_broadcast([P, 12, 4, LIST_ROWS]),
+            out=spread[0][:].rearrange("p (s g r) -> p s g r", g=2, r=LIST_ROWS),
+            in_=turned[0][:].rearrange("p (g s) -> p s g", s=LIST_ROWS).unsqueeze(3).to_broadcast([P, LIST_ROWS, 2, LIST_ROWS]),
         )
         nc.vector.tensor_copy(
             out=w_codes[:].bitcast(U16).rearrange("p (t m) -> p t m", t=PACK),
             in_=raw_words[:].bitcast(U16).rearrange("p (m t) -> p t m", t=PACK),
         )
-        nc.vector.transpose(weights[:, HALF : 2 * J], spread[:])
+        nc.vector.transpose(weights[:, 0:J], spread[0][:])
+        turned_banks = []
+        for h in range(2):
+            nc.scalar.copy(
+                out=spread[1][:, h * HALF : (h + 1) * HALF].rearrange("p (g r) -> p g r", r=LIST_ROWS),
+                in_=turned[1][:, 16 * h : 16 * h + 16].unsqueeze(2).to_broadcast([P, 16, LIST_ROWS]),
+            )
+            turned_banks.append(psum.tile([P, 2, P], F32, name="bank", tag="bank"))
+            for c in range(2):
+                at = h * HALF + c * P
+                nc.tensor.transpose(turned_banks[h][:, c, :], spread[1][:, at : at + P], identity[:])
+        for h in range(2):
+            nc.scalar.copy(
+                out=weights[:, J : 2 * J].rearrange("p (q c j) -> p c q j", q=4, c=4)[:, 2 * h : 2 * h + 2, :, :],
+                in_=turned_banks[h][:].rearrange("p c (q j) -> p c q j", q=4),
+            )
 
         def gather(dst, i, c, j0, width):
             first = c * J + j0
@@ -125,7 +143,7 @@ def tile_list_max_geluP_kernel(tc, xT, wgt, w_words, w_scales, b, offs, out_0, o
             nc.scalar.copy(out=first[k][:], in_=bank[:])
 
         flat = rows[:].rearrange("p r j -> p (r j)")
-        late = PACK * HALF + PIECE
+        late = PACK * HALF + PIECE + 64
 
         def freed(at):
             return flat[:, at : at + J].rearrange("p (t j) -> p t j", t=PACK)
@@ -137,15 +155,15 @@ def tile_list_max_geluP_kernel(tc, xT, wgt, w_words, w_scales, b, offs, out_0, o
 
         def max_of_two(k):
             second = project(operands[1], k * PIECE)
-            if k == 2:
-                of_two[k] = freed(late)
+            if k >= 2:
+                of_two[k] = freed(late + (k - 2) * J)
             else:
                 of_two[k] = keep.tile([P, PACK, PIECE], F32, name="of_two%d" % k)[:]
             seconds[k] = second
             part_of_two(k, 0, 2 if k == 3 else PACK)
 
         def max_of_three(k):
-            third = project(operands[2, max(k, 1)], PIECE if k == 1 else 0)
+            third = project(operands[2, k // 2], (k % 2) * PIECE)
             if k == 1:
                 of_three[k] = freed(late - J)
             else:
@@ -167,10 +185,8 @@ def tile_list_max_geluP_kernel(tc, xT, wgt, w_words, w_scales, b, offs, out_0, o
             nc.sync.dma_start(out=out_rows[:, :, j0 : j0 + PIECE], in_=y[:])
             return y
 
-        def round_on_pool(y, k):
-            nc.gpsimd.tensor_scalar(
-                y_rounded[0][:, k * PIECE : (k + 1) * PIECE, :], y[:].rearrange("p t j -> p j t"), 1.0, 0.0, MULT, ADD
-            )
+        def round_on_pool(dst, src):
+            nc.gpsimd.tensor_scalar(dst, src.rearrange("p i j -> p j i"), 1.0, 0.0, MULT, ADD)
 
         def round_y(copy, y, k, lo, hi):
             at = (k % 2) * PIECE
@@ -191,7 +207,9 @@ def tile_list_max_geluP_kernel(tc, xT, wgt, w_words, w_scales, b, offs, out_0, o
             if at + width == HALF:
                 nc.sync.dma_start(out=out_words[:, j0 - at : j0 - at + HALF], in_=y_codes[j0 // HALF][:].bitcast(I32))
 
-        for i in range(3):
+        for c in range(2):
+            gather(picked[:, 0, c * J : (c + 1) * J], 0, c, 0, J)
+        for i in (1, 2):
             gather(picked[:, i, :], i, 0, 0, 2 * J)
         nc.vector.tensor_copy(
             out=w_plane[:].rearrange("p (t m) -> p t m", t=PACK),
@@ -209,19 +227,17 @@ def tile_list_max_geluP_kernel(tc, xT, wgt, w_words, w_scales, b, offs, out_0, o
             for i in range(PACK):
                 gather(rows[:, PACK * h + i, :], i, 2, h * HALF, HALF)
         round_rows(2, 0, rows[:, 0:PACK, :])
-        operands[2, 1] = quantize(rounded[2][:, 0:HALF, :], HALF, "2_1")
+        operands[2, 0] = quantize(rounded[2][:, 0:HALF, :], HALF, "2_0")
         for k in range(3):
             hold_first(k)
         for k in (0, 1):
             max_of_two(k)
         max_of_three(0)
-        for k in (2, 3):
-            at = (k - 2) * PIECE
-            round_rows(2, k * PIECE, rows[:, PACK : 2 * PACK, at : at + PIECE])
+        round_rows(2, HALF, rows[:, PACK : 2 * PACK, 0:PIECE])
+        round_on_pool(rounded[2][:, J - PIECE : J, :], rows[:, PACK : 2 * PACK, PIECE:])
         hold_first(3)
-        operands[2, 2] = quantize(rounded[2][:, 2 * PIECE : 3 * PIECE, :], PIECE, "2_2")
+        operands[2, 1] = quantize(rounded[2][:, HALF:J, :], HALF, "2_1")
         max_of_three(1)
-        operands[2, 3] = quantize(rounded[2][:, 3 * PIECE : J, :], PIECE, "2_3")
         max_of_two(2)
         max_of_two(3)
         max_of_three(2)
@@ -229,11 +245,11 @@ def tile_list_max_geluP_kernel(tc, xT, wgt, w_words, w_scales, b, offs, out_0, o
         max_of_three(3)
         ys = {k: finish(k) for k in (0, 1)}
         for k in (0, 1):
-            round_on_pool(ys[k], k)
+            round_on_pool(y_rounded[0][:, k * PIECE : (k + 1) * PIECE, :], ys[k][:])
         for k in (2, 3):
             ys[k] = finish(k)
-        round_y(nc.vector.tensor_copy, ys[2], 2, 0, PIECE)
         hand_on(0, HALF)
+        round_y(nc.vector.tensor_copy, ys[2], 2, 0, PIECE)
         hand_on(HALF, PIECE)
         round_y(nc.scalar.copy, ys[3], 3, 0, PIECE // 2)
         round_y(nc.vector.tensor_copy, ys[3], 3, PIECE // 2, PIECE)

@@ -160,7 +160,7 @@ def tile_list_max_geluP_kernel(tc, xT, wgt, w_words, w_scales, b, offs, out_0, o
             else:
                 of_two[k] = keep.tile([P, PACK, PIECE], F32, name="of_two%d" % k)[:]
             seconds[k] = second
-            part_of_two(k, 0, 2 if k == 3 else PACK)
+            part_of_two(k, 0, 2 if k >= 2 else PACK)
 
         def max_of_three(k):
             third = project(operands[2, k // 2], (k % 2) * PIECE)
@@ -168,7 +168,9 @@ def tile_list_max_geluP_kernel(tc, xT, wgt, w_words, w_scales, b, offs, out_0, o
                 of_three[k] = freed(late - J)
             else:
                 of_three[k] = keep.tile([P, PACK, PIECE], F32, name="of_three%d" % k)[:]
-            for t0, t1 in ((0, 2), (2, 4)) if k == 3 else ((0, 4),):
+            step = (PACK, PACK, 2, 1)[k]
+            for t0 in range(0, PACK, step):
+                t1 = t0 + step
                 nc.vector.tensor_tensor(of_three[k][:, t0:t1, :], third[:, t0:t1, :], of_two[k][:, t0:t1, :], MAX)
 
         y_plane = keep.tile([P, J], U8, name="y_plane", align_bytes=64)
@@ -239,8 +241,9 @@ def tile_list_max_geluP_kernel(tc, xT, wgt, w_words, w_scales, b, offs, out_0, o
         operands[2, 1] = quantize(rounded[2][:, HALF:J, :], HALF, "2_1")
         max_of_three(1)
         max_of_two(2)
-        max_of_two(3)
+        part_of_two(2, 2, PACK)
         max_of_three(2)
+        max_of_two(3)
         part_of_two(3, 2, PACK)
         max_of_three(3)
         ys = {k: finish(k) for k in (0, 1)}
@@ -248,11 +251,11 @@ def tile_list_max_geluP_kernel(tc, xT, wgt, w_words, w_scales, b, offs, out_0, o
             round_on_pool(y_rounded[0][:, k * PIECE : (k + 1) * PIECE, :], ys[k][:])
         for k in (2, 3):
             ys[k] = finish(k)
-        hand_on(0, HALF)
         round_y(nc.vector.tensor_copy, ys[2], 2, 0, PIECE)
-        hand_on(HALF, PIECE)
+        hand_on(0, HALF)
         round_y(nc.scalar.copy, ys[3], 3, 0, PIECE // 2)
         round_y(nc.vector.tensor_copy, ys[3], 3, PIECE // 2, PIECE)
+        hand_on(HALF, PIECE)
         hand_on(HALF + PIECE, PIECE)
         for q in range(4):
             queue = nc.scalar if q % 2 else nc.sync

@@ -47,8 +47,8 @@ def tile_list_max_geluP_kernel(tc, xT, wgt, w_words, w_scales, b, offs, out_0, o
         warm = keep.tile([P, 8], F32, name="warm")
         warm2 = keep.tile([P, 8], F32, name="warm2")
 
-        nc.vector.memset(warm[:], 0.0)
         nc.vector.memset(raw_scales[:].bitcast(I32), 0)
+        nc.vector.memset(warm[:], 0.0)
         x_rows = xT.rearrange("(p i) t -> p i t", i=PACK)
         make_identity(nc, identity[:])
         head_rows = wgt.rearrange("(h r) c -> h r c", r=LIST_ROWS)[:, 0, :]
@@ -56,10 +56,9 @@ def tile_list_max_geluP_kernel(tc, xT, wgt, w_words, w_scales, b, offs, out_0, o
         nc.sync.dma_start(out=seeds[1][:], in_=head_rows[:, J : 2 * J].rearrange("h (u c) -> u h c", c=SEED))
         nc.sync.dma_start(out=raw_words[:].bitcast(I32), in_=w_words[0].bitcast(I32))
         nc.sync.dma_start(out=offsets[:], in_=offs)
+        nc.sync.dma_start(out=raw_scales[0:16, :].bitcast(I32), in_=w_scales[0].bitcast(I32))
         nc.sync.dma_start(out=planes[0][:], in_=x_rows[:, 0, :])
         nc.sync.dma_start(out=planes[1][:], in_=x_rows[:, 1, :])
-        for q in range(4):
-            nc.sync.dma_start(out=raw_scales[32 * q : 32 * q + 4, :].bitcast(I32), in_=w_scales[0, 4 * q : 4 * q + 4, :].bitcast(I32))
         nc.sync.dma_start(out=planes[2][:], in_=x_rows[:, 2, :])
         nc.sync.dma_start(out=planes[3][:], in_=x_rows[:, 3, :])
         nc.sync.dma_start(out=weights[:, 2 * J :], in_=wgt[:, 2 * J :])
@@ -79,6 +78,12 @@ def tile_list_max_geluP_kernel(tc, xT, wgt, w_words, w_scales, b, offs, out_0, o
             in_=raw_words[:].bitcast(U16).rearrange("p (m t) -> p t m", t=PACK),
         )
         nc.vector.transpose(weights[:, 0:J], spread[0][:])
+        nc.vector.tensor_copy(
+            out=w_plane[:].rearrange("p (t m) -> p t m", t=PACK),
+            in_=raw_scales[:].rearrange("p (m t) -> p t m", t=PACK),
+        )
+        for q in range(1, 4):
+            nc.sync.dma_start(out=w_plane[32 * q : 32 * q + 4, :].bitcast(I32), in_=w_plane[4 * q : 4 * q + 4, :].bitcast(I32))
         turned_banks = []
         for h in range(2):
             nc.scalar.copy(
@@ -160,7 +165,7 @@ def tile_list_max_geluP_kernel(tc, xT, wgt, w_words, w_scales, b, offs, out_0, o
             else:
                 of_two[k] = keep.tile([P, PACK, PIECE], F32, name="of_two%d" % k)[:]
             seconds[k] = second
-            part_of_two(k, 0, 2 if k >= 2 else PACK)
+            part_of_two(k, 0, 2 if k == 3 else PACK)
 
         def max_of_three(k):
             third = project(operands[2, k // 2], (k % 2) * PIECE)
@@ -168,7 +173,7 @@ def tile_list_max_geluP_kernel(tc, xT, wgt, w_words, w_scales, b, offs, out_0, o
                 of_three[k] = freed(late - J)
             else:
                 of_three[k] = keep.tile([P, PACK, PIECE], F32, name="of_three%d" % k)[:]
-            step = (PACK, PACK, 2, 1)[k]
+            step = (PACK, PACK, PACK, 1)[k]
             for t0 in range(0, PACK, step):
                 t1 = t0 + step
                 nc.vector.tensor_tensor(of_three[k][:, t0:t1, :], third[:, t0:t1, :], of_two[k][:, t0:t1, :], MAX)
@@ -213,10 +218,6 @@ def tile_list_max_geluP_kernel(tc, xT, wgt, w_words, w_scales, b, offs, out_0, o
             gather(picked[:, 0, c * J : (c + 1) * J], 0, c, 0, J)
         for i in (1, 2):
             gather(picked[:, i, :], i, 0, 0, 2 * J)
-        nc.vector.tensor_copy(
-            out=w_plane[:].rearrange("p (t m) -> p t m", t=PACK),
-            in_=raw_scales[:].rearrange("p (m t) -> p t m", t=PACK),
-        )
         for j0, j1 in ((0, PIECE), (PIECE, J), (J, 2 * J)):
             gather(picked[:, 3, j0:j1], 3, 0, j0, j1 - j0)
         for j0, j1 in ((0, PIECE), (PIECE, HALF), (HALF, J)):
@@ -239,9 +240,8 @@ def tile_list_max_geluP_kernel(tc, xT, wgt, w_words, w_scales, b, offs, out_0, o
         round_on_pool(rounded[2][:, J - PIECE : J, :], rows[:, PACK : 2 * PACK, PIECE:])
         hold_first(3)
         operands[2, 1] = quantize(rounded[2][:, HALF:J, :], HALF, "2_1")
-        max_of_three(1)
         max_of_two(2)
-        part_of_two(2, 2, PACK)
+        max_of_three(1)
         max_of_three(2)
         max_of_two(3)
         part_of_two(3, 2, PACK)

@@ -37,9 +37,10 @@ def tile_list_max_geluP_kernel(tc, xT, wgt, w_words, w_scales, b, offs, out_0, o
         offsets = keep.tile([P, PICKS * J // LIST_ROWS], U16, name="offsets")
         planes = [keep.tile([P, T], F32, name="plane%d" % i) for i in range(PACK)]
         weights = keep.tile([P, PICKS * J], F32, name="weights", align_bytes=64)
-        seeds = [keep.tile([P, SEED], F32, name="seeds%d" % c, align_bytes=64) for c in range(2)]
-        turned = [keep.tile([P, SEED], F32, name="turned%d" % c, align_bytes=64) for c in range(2)]
-        spread = [keep.tile([P, J], F32, name="spread%d" % c, align_bytes=64) for c in range(2)]
+        seeds = [keep.tile([P, SEED * (c + 1)], F32, name="seeds%d" % c, align_bytes=64) for c in range(2)]
+        turned = [keep.tile([P, SEED * (c + 1)], F32, name="turned%d" % c, align_bytes=64) for c in range(2)]
+        spread = [keep.tile([P, J], F32, name="spread0", align_bytes=64)]
+        spread.extend([keep.tile([P, HALF], F32, name="spread1_%d" % n) for n in range(4)])
         identity = keep.tile([P, P], F32, name="identity")
         raw_words = keep.tile([P, 2 * N], U8, name="raw_words")
         raw_scales = keep.tile([P, N], U8, name="raw_scales")
@@ -53,7 +54,7 @@ def tile_list_max_geluP_kernel(tc, xT, wgt, w_words, w_scales, b, offs, out_0, o
         make_identity(nc, identity[:])
         head_rows = wgt.rearrange("(h r) c -> h r c", r=LIST_ROWS)[:, 0, :]
         nc.sync.dma_start(out=seeds[0][:], in_=head_rows[:, 0:J].rearrange("h (s c) -> h s c", c=SEED))
-        nc.sync.dma_start(out=seeds[1][:], in_=head_rows[:, J : 2 * J].rearrange("h (u c) -> u h c", c=SEED))
+        nc.sync.dma_start(out=seeds[1][:], in_=head_rows[:, J:].rearrange("h (u c) -> u h c", c=2 * SEED))
         nc.sync.dma_start(out=raw_words[:].bitcast(I32), in_=w_words[0].bitcast(I32))
         nc.sync.dma_start(out=offsets[:], in_=offs)
         nc.sync.dma_start(out=raw_scales[0:16, :].bitcast(I32), in_=w_scales[0].bitcast(I32))
@@ -61,12 +62,12 @@ def tile_list_max_geluP_kernel(tc, xT, wgt, w_words, w_scales, b, offs, out_0, o
         nc.sync.dma_start(out=planes[1][:], in_=x_rows[:, 1, :])
         nc.sync.dma_start(out=planes[2][:], in_=x_rows[:, 2, :])
         nc.sync.dma_start(out=planes[3][:], in_=x_rows[:, 3, :])
-        nc.sync.dma_start(out=weights[:, 2 * J :], in_=wgt[:, 2 * J :])
         nc.sync.dma_start(out=bias[:], in_=b.rearrange("(p t) -> p t", t=PACK))
         nc.scalar.activation(out=warm2[:], in_=warm[:], func=GELU)
 
-        for c in range(2):
-            nc.vector.transpose(turned[c][:], seeds[c][:])
+        nc.vector.transpose(turned[0][:], seeds[0][:])
+        for at in (0, SEED):
+            nc.vector.transpose(turned[1][:, at : at + SEED], seeds[1][:, at : at + SEED])
         w_codes = keep.tile([P, 2 * N], U8, name="w_codes", align_bytes=64)
         w_plane = keep.tile([P, N], U8, name="w_plane", align_bytes=64)
         nc.vector.tensor_copy(
@@ -85,19 +86,20 @@ def tile_list_max_geluP_kernel(tc, xT, wgt, w_words, w_scales, b, offs, out_0, o
         for q in range(1, 4):
             nc.sync.dma_start(out=w_plane[32 * q : 32 * q + 4, :].bitcast(I32), in_=w_plane[4 * q : 4 * q + 4, :].bitcast(I32))
         turned_banks = []
-        for h in range(2):
-            nc.scalar.copy(
-                out=spread[1][:, h * HALF : (h + 1) * HALF].rearrange("p (g r) -> p g r", r=LIST_ROWS),
-                in_=turned[1][:, 16 * h : 16 * h + 16].unsqueeze(2).to_broadcast([P, 16, LIST_ROWS]),
+        for n in range(4):
+            copy = nc.scalar.copy if n < 2 else nc.vector.tensor_copy
+            copy(
+                out=spread[1 + n][:].rearrange("p (g r) -> p g r", r=LIST_ROWS),
+                in_=turned[1][:, 16 * n : 16 * n + 16].unsqueeze(2).to_broadcast([P, 16, LIST_ROWS]),
             )
             turned_banks.append(psum.tile([P, 2, P], F32, name="bank", tag="bank"))
             for c in range(2):
-                at = h * HALF + c * P
-                nc.tensor.transpose(turned_banks[h][:, c, :], spread[1][:, at : at + P], identity[:])
-        for h in range(2):
+                nc.tensor.transpose(turned_banks[n][:, c, :], spread[1 + n][:, c * P : (c + 1) * P], identity[:])
+        built = weights[:, J:].rearrange("p (q u b j) -> p b u q j", q=4, u=4, b=2)
+        for n in range(4):
             nc.scalar.copy(
-                out=weights[:, J : 2 * J].rearrange("p (q c j) -> p c q j", q=4, c=4)[:, 2 * h : 2 * h + 2, :, :],
-                in_=turned_banks[h][:].rearrange("p c (q j) -> p c q j", q=4),
+                out=built[:, n // 2, 2 * (n % 2) : 2 * (n % 2) + 2, :, :],
+                in_=turned_banks[n][:].rearrange("p c (q j) -> p c q j", q=4),
             )
 
         def gather(dst, i, c, j0, width):
@@ -126,8 +128,11 @@ def tile_list_max_geluP_kernel(tc, xT, wgt, w_words, w_scales, b, offs, out_0, o
                 )
             return bank
 
-        rows = keep.tile([P, 2 + 4 * PACK, HALF], F32, name="rows")
-        picked = rows[:, 2:, :].rearrange("p (i u) j -> p i (u j)", i=PACK)
+        EARLY = 2 * J + PIECE
+        LATE = J - PIECE
+        flat = keep.tile([P, HALF + PACK * EARLY], F32, name="flat")
+        picked = flat[:, HALF:].rearrange("p (i j) -> p i j", i=PACK)
+        late = flat[:, 0 : PACK * LATE].rearrange("p (i j) -> p i j", i=PACK)
         operands = {}
         first = {}
         of_two = {}
@@ -147,9 +152,6 @@ def tile_list_max_geluP_kernel(tc, xT, wgt, w_words, w_scales, b, offs, out_0, o
             first[k] = keep.tile([P, PACK, PIECE], F32, name="first%d" % k)
             nc.scalar.copy(out=first[k][:], in_=bank[:])
 
-        flat = rows[:].rearrange("p r j -> p (r j)")
-        late = PACK * HALF + PIECE + 64
-
         def freed(at):
             return flat[:, at : at + J].rearrange("p (t j) -> p t j", t=PACK)
 
@@ -161,16 +163,16 @@ def tile_list_max_geluP_kernel(tc, xT, wgt, w_words, w_scales, b, offs, out_0, o
         def max_of_two(k):
             second = project(operands[1], k * PIECE)
             if k >= 2:
-                of_two[k] = freed(late + (k - 2) * J)
+                of_two[k] = freed((k - 1) * J)
             else:
                 of_two[k] = keep.tile([P, PACK, PIECE], F32, name="of_two%d" % k)[:]
             seconds[k] = second
             part_of_two(k, 0, 2 if k == 3 else PACK)
 
         def max_of_three(k):
-            third = project(operands[2, k // 2], (k % 2) * PIECE)
+            third = project(operands[2, min(k, 2)], PIECE if k == 3 else 0)
             if k == 1:
-                of_three[k] = freed(late - J)
+                of_three[k] = freed(0)
             else:
                 of_three[k] = keep.tile([P, PACK, PIECE], F32, name="of_three%d" % k)[:]
             step = (PACK, PACK, PACK, 1)[k]
@@ -189,7 +191,8 @@ def tile_list_max_geluP_kernel(tc, xT, wgt, w_words, w_scales, b, offs, out_0, o
             y = keep.tile([P, PACK, PIECE], F32, name="y%d" % k)
             for t in range(PACK):
                 nc.scalar.activation(out=y[:, t, :], in_=of_three[k][:, t, :], func=GELU, bias=bias[:, t : t + 1])
-            nc.sync.dma_start(out=out_rows[:, :, j0 : j0 + PIECE], in_=y[:])
+            for t0, t1 in ((0, 2), (2, 4)) if k == 1 else ((0, 4),):
+                nc.sync.dma_start(out=out_rows[:, t0:t1, j0 : j0 + PIECE], in_=y[:, t0:t1, :])
             return y
 
         def round_on_pool(dst, src):
@@ -214,32 +217,34 @@ def tile_list_max_geluP_kernel(tc, xT, wgt, w_words, w_scales, b, offs, out_0, o
             if at + width == HALF:
                 nc.sync.dma_start(out=out_words[:, j0 - at : j0 - at + HALF], in_=y_codes[j0 // HALF][:].bitcast(I32))
 
-        for c in range(2):
-            gather(picked[:, 0, c * J : (c + 1) * J], 0, c, 0, J)
+        for j0, j1 in ((0, J), (J, EARLY)):
+            gather(picked[:, 0, j0:j1], 0, 0, j0, j1 - j0)
         for i in (1, 2):
-            gather(picked[:, i, :], i, 0, 0, 2 * J)
-        for j0, j1 in ((0, PIECE), (PIECE, J), (J, 2 * J)):
+            gather(picked[:, i, :], i, 0, 0, EARLY)
+        for j0, j1 in ((0, PIECE), (PIECE, J), (J, EARLY)):
             gather(picked[:, 3, j0:j1], 3, 0, j0, j1 - j0)
         for j0, j1 in ((0, PIECE), (PIECE, HALF), (HALF, J)):
             round_rows(0, j0, picked[:, :, j0:j1])
         operands[0] = quantize(rounded[0][:, 0:J, :], J, "0")
-        for j0 in (0, HALF):
-            round_rows(1, j0, picked[:, :, J + j0 : J + j0 + HALF])
+        for j0, j1 in ((0, LATE), (LATE, J)):
+            round_rows(1, j0, picked[:, :, J + j0 : J + j1])
         operands[1] = quantize(rounded[1][:, 0:J, :], J, "1")
-        for h in range(2):
-            for i in range(PACK):
-                gather(rows[:, PACK * h + i, :], i, 2, h * HALF, HALF)
-        round_rows(2, 0, rows[:, 0:PACK, :])
-        operands[2, 0] = quantize(rounded[2][:, 0:HALF, :], HALF, "2_0")
-        for k in range(3):
+        round_rows(2, 0, picked[:, :, 2 * J :])
+        operands[2, 0] = quantize(rounded[2][:, 0:PIECE, :], PIECE, "2_0")
+        for i in range(PACK):
+            gather(late[:, i, :], i, 2, PIECE, LATE)
+        for k in (0, 1):
             hold_first(k)
         for k in (0, 1):
             max_of_two(k)
         max_of_three(0)
-        round_rows(2, HALF, rows[:, PACK : 2 * PACK, 0:PIECE])
-        round_on_pool(rounded[2][:, J - PIECE : J, :], rows[:, PACK : 2 * PACK, PIECE:])
-        hold_first(3)
-        operands[2, 1] = quantize(rounded[2][:, HALF:J, :], HALF, "2_1")
+        round_rows(2, PIECE, late[:, :, 0:PIECE])
+        round_rows(2, HALF, late[:, :, PIECE:HALF])
+        round_on_pool(rounded[2][:, J - PIECE : J, :], late[:, :, HALF:])
+        for k in (2, 3):
+            hold_first(k)
+        operands[2, 1] = quantize(rounded[2][:, PIECE:HALF, :], PIECE, "2_1")
+        operands[2, 2] = quantize(rounded[2][:, HALF:J, :], HALF, "2_2")
         max_of_two(2)
         max_of_three(1)
         max_of_three(2)

@@ -87,8 +87,7 @@ def tile_list_max_geluP_kernel(tc, xT, wgt, w_words, w_scales, b, offs, out_0, o
             nc.sync.dma_start(out=w_plane[32 * q : 32 * q + 4, :].bitcast(I32), in_=w_plane[4 * q : 4 * q + 4, :].bitcast(I32))
         turned_banks = []
         for n in range(4):
-            copy = nc.scalar.copy if n < 2 else nc.vector.tensor_copy
-            copy(
+            nc.scalar.copy(
                 out=spread[1 + n][:].rearrange("p (g r) -> p g r", r=LIST_ROWS),
                 in_=turned[1][:, 16 * n : 16 * n + 16].unsqueeze(2).to_broadcast([P, 16, LIST_ROWS]),
             )
@@ -96,11 +95,12 @@ def tile_list_max_geluP_kernel(tc, xT, wgt, w_words, w_scales, b, offs, out_0, o
             for c in range(2):
                 nc.tensor.transpose(turned_banks[n][:, c, :], spread[1 + n][:, c * P : (c + 1) * P], identity[:])
         built = weights[:, J:].rearrange("p (q u b j) -> p b u q j", q=4, u=4, b=2)
-        for n in range(4):
-            nc.scalar.copy(
-                out=built[:, n // 2, 2 * (n % 2) : 2 * (n % 2) + 2, :, :],
-                in_=turned_banks[n][:].rearrange("p c (q j) -> p c q j", q=4),
-            )
+        for q0 in (0, 2):
+            for n in range(4):
+                nc.scalar.copy(
+                    out=built[:, n // 2, 2 * (n % 2) : 2 * (n % 2) + 2, q0 : q0 + 2, :],
+                    in_=turned_banks[n][:].rearrange("p c (q j) -> p c q j", q=4)[:, :, q0 : q0 + 2, :],
+                )
 
         def gather(dst, i, c, j0, width):
             first = c * J + j0
@@ -148,7 +148,7 @@ def tile_list_max_geluP_kernel(tc, xT, wgt, w_words, w_scales, b, offs, out_0, o
             )
 
         def hold_first(k):
-            bank = project(operands[0], k * PIECE)
+            bank = project(operands[0, k // 2], (k % 2) * PIECE)
             first[k] = keep.tile([P, PACK, PIECE], F32, name="first%d" % k)
             nc.scalar.copy(out=first[k][:], in_=bank[:])
 
@@ -217,7 +217,7 @@ def tile_list_max_geluP_kernel(tc, xT, wgt, w_words, w_scales, b, offs, out_0, o
             if at + width == HALF:
                 nc.sync.dma_start(out=out_words[:, j0 - at : j0 - at + HALF], in_=y_codes[j0 // HALF][:].bitcast(I32))
 
-        for j0, j1 in ((0, J), (J, EARLY)):
+        for j0, j1 in ((0, J), (J, 2 * J), (2 * J, EARLY)):
             gather(picked[:, 0, j0:j1], 0, 0, j0, j1 - j0)
         for i in (1, 2):
             gather(picked[:, i, :], i, 0, 0, EARLY)
@@ -225,7 +225,8 @@ def tile_list_max_geluP_kernel(tc, xT, wgt, w_words, w_scales, b, offs, out_0, o
             gather(picked[:, 3, j0:j1], 3, 0, j0, j1 - j0)
         for j0, j1 in ((0, PIECE), (PIECE, HALF), (HALF, J)):
             round_rows(0, j0, picked[:, :, j0:j1])
-        operands[0] = quantize(rounded[0][:, 0:J, :], J, "0")
+        for h in range(2):
+            operands[0, h] = quantize(rounded[0][:, h * HALF : (h + 1) * HALF, :], HALF, "0_%d" % h)
         for j0, j1 in ((0, LATE), (LATE, J)):
             round_rows(1, j0, picked[:, :, J + j0 : J + j1])
         operands[1] = quantize(rounded[1][:, 0:J, :], J, "1")
@@ -233,16 +234,14 @@ def tile_list_max_geluP_kernel(tc, xT, wgt, w_words, w_scales, b, offs, out_0, o
         operands[2, 0] = quantize(rounded[2][:, 0:PIECE, :], PIECE, "2_0")
         for i in range(PACK):
             gather(late[:, i, :], i, 2, PIECE, LATE)
-        for k in (0, 1):
+        for k in range(3):
             hold_first(k)
         for k in (0, 1):
             max_of_two(k)
         max_of_three(0)
-        round_rows(2, PIECE, late[:, :, 0:PIECE])
-        round_rows(2, HALF, late[:, :, PIECE:HALF])
-        round_on_pool(rounded[2][:, J - PIECE : J, :], late[:, :, HALF:])
-        for k in (2, 3):
-            hold_first(k)
+        round_rows(2, PIECE, late[:, :, 0 : LATE // 2])
+        round_on_pool(rounded[2][:, J - LATE // 2 : J, :], late[:, :, LATE // 2 :])
+        hold_first(3)
         operands[2, 1] = quantize(rounded[2][:, PIECE:HALF, :], PIECE, "2_1")
         operands[2, 2] = quantize(rounded[2][:, HALF:J, :], HALF, "2_2")
         max_of_two(2)

@@ -175,7 +175,7 @@ def tile_list_max_geluP_kernel(tc, xT, wgt, w_words, w_scales, b, offs, out_0, o
                 of_three[k] = freed(0)
             else:
                 of_three[k] = keep.tile([P, PACK, PIECE], F32, name="of_three%d" % k)[:]
-            step = (PACK, PACK, PACK, 1)[k]
+            step = (PACK, 2, 2, 1)[k]
             for t0 in range(0, PACK, step):
                 t1 = t0 + step
                 nc.vector.tensor_tensor(of_three[k][:, t0:t1, :], third[:, t0:t1, :], of_two[k][:, t0:t1, :], MAX)

from contextlib import ExitStack

import concourse.mybir as mybir
from concourse.masks import make_identity

K, N, T, J = 512, 512, 2048, 512
PICKS = 3
FLOPS = 2 * K * N * J * PICKS

F32 = mybir.dt.float32
BF16 = mybir.dt.bfloat16
I32 = mybir.dt.int32
U32 = mybir.dt.uint32
U16 = mybir.dt.uint16
U8 = mybir.dt.uint8
FP8X4 = mybir.dt.float8_e4m3fn_x4
FP4X4 = mybir.dt.float4_e2m1fn_x4
MULT = mybir.AluOpType.mult
MAX = mybir.AluOpType.max
ADD = mybir.AluOpType.add
GELU = mybir.ActivationFunctionType.Gelu_apprx_tanh

P = 128
PACK = 4
PIECE = 128
HALF = 256
LIST_ROWS = 16
SEED = 32


def tile_list_max_geluP_kernel(tc, xT, wgt, w_words, w_scales, b, offs, out_0, out_1, out_2):
    nc = tc.nc
    with ExitStack() as ctx:
        keep = ctx.enter_context(tc.tile_pool(name="keep", bufs=1))
        psum = ctx.enter_context(tc.psum_pool(name="psum", bufs=8))

        offsets = keep.tile([P, PICKS * J // LIST_ROWS], U16, name="offsets")
        planes = [keep.tile([P, T], F32, name="plane%d" % i) for i in range(PACK)]
        weights = keep.tile([P, PICKS * J], F32, name="weights", align_bytes=64)
        seeds = [keep.tile([P, SEED * (c + 1)], F32, name="seeds%d" % c, align_bytes=64) for c in range(2)]
        turned = [keep.tile([P, SEED * (c + 1)], F32, name="turned%d" % c, align_bytes=64) for c in range(2)]
        spread = [keep.tile([P, J], F32, name="spread0", align_bytes=64)]
        spread.extend([keep.tile([P, HALF], F32, name="spread1_%d" % n) for n in range(4)])
        identity = keep.tile([P, P], F32, name="identity")
        raw_words = keep.tile([P, 2 * N], U8, name="raw_words")
        raw_scales = keep.tile([P, N], U8, name="raw_scales")
        bias = keep.tile([P, PACK], F32, name="bias")
        warm = keep.tile([P, 8], F32, name="warm")
        warm2 = keep.tile([P, 8], F32, name="warm2")

        nc.vector.memset(raw_scales[:].bitcast(I32), 0)
        nc.vector.memset(warm[:], 0.0)
        x_rows = xT.rearrange("(p i) t -> p i t", i=PACK)
        make_identity(nc, identity[:])
        head_rows = wgt.rearrange("(h r) c -> h r c", r=LIST_ROWS)[:, 0, :]
        nc.sync.dma_start(out=seeds[0][:], in_=head_rows[:, 0:J].rearrange("h (s c) -> h s c", c=SEED))
        nc.sync.dma_start(out=seeds[1][:], in_=head_rows[:, J:].rearrange("h (u c) -> u h c", c=2 * SEED))
        nc.sync.dma_start(out=raw_words[:].bitcast(I32), in_=w_words[0].bitcast(I32))
        nc.sync.dma_start(out=offsets[:], in_=offs)
        nc.sync.dma_start(out=raw_scales[0:16, :].bitcast(I32), in_=w_scales[0].bitcast(I32))
        nc.sync.dma_start(out=planes[0][:], in_=x_rows[:, 0, :])
        nc.sync.dma_start(out=planes[1][:], in_=x_rows[:, 1, :])
        nc.sync.dma_start(out=planes[2][:], in_=x_rows[:, 2, :])
        nc.sync.dma_start(out=planes[3][:], in_=x_rows[:, 3, :])
        nc.sync.dma_start(out=bias[:], in_=b.rearrange("(p t) -> p t", t=PACK))
        nc.scalar.activation(out=warm2[:], in_=warm[:], func=GELU)

        nc.vector.transpose(turned[0][:], seeds[0][:])
        for at in (0, SEED):
            nc.vector.transpose(turned[1][:, at : at + SEED], seeds[1][:, at : at + SEED])
        w_codes = keep.tile([P, 2 * N], U8, name="w_codes", align_bytes=64)
        w_plane = keep.tile([P, N], U8, name="w_plane", align_bytes=64)
        nc.vector.tensor_copy(
            out=spread[0][:].rearrange("p (s g r) -> p s g r", g=2, r=LIST_ROWS),
            in_=turned[0][:].rearrange("p (g s) -> p s g", s=LIST_ROWS).unsqueeze(3).to_broadcast([P, LIST_ROWS, 2, LIST_ROWS]),
        )
        nc.vector.tensor_copy(
            out=w_codes[:].bitcast(U16).rearrange("p (t m) -> p t m", t=PACK),
            in_=raw_words[:].bitcast(U16).rearrange("p (m t) -> p t m", t=PACK),
        )
        nc.vector.transpose(weights[:, 0:J], spread[0][:])
        nc.vector.tensor_copy(
            out=w_plane[:].rearrange("p (t m) -> p t m", t=PACK),
            in_=raw_scales[:].rearrange("p (m t) -> p t m", t=PACK),
        )
        for q in range(1, 4):
            nc.sync.dma_start(out=w_plane[32 * q : 32 * q + 4, :].bitcast(I32), in_=w_plane[4 * q : 4 * q + 4, :].bitcast(I32))
        turned_banks = []
        for n in range(4):
            nc.scalar.copy(
                out=spread[1 + n][:].rearrange("p (g r) -> p g r", r=LIST_ROWS),
                in_=turned[1][:, 16 * n : 16 * n + 16].unsqueeze(2).to_broadcast([P, 16, LIST_ROWS]),
            )
            turned_banks.append(psum.tile([P, 2, P], F32, name="bank", tag="bank"))
            for c in range(2):
                nc.tensor.transpose(turned_banks[n][:, c, :], spread[1 + n][:, c * P : (c + 1) * P], identity[:])
        built = weights[:, J:].rearrange("p (q u b j) -> p b u q j", q=4, u=4, b=2)
        for q0 in (0, 2):
            for n in range(4):
                nc.scalar.copy(
                    out=built[:, n // 2, 2 * (n % 2) : 2 * (n % 2) + 2, q0 : q0 + 2, :],
                    in_=turned_banks[n][:].rearrange("p c (q j) -> p c q j", q=4)[:, :, q0 : q0 + 2, :],
                )

        def gather(dst, i, c, j0, width):
            first = c * J + j0
            picks = offsets[:, first // LIST_ROWS : (first + width) // LIST_ROWS]
            nc.vector.tensor_tensor(dst, planes[i][:].indirect(picks), weights[:, first : first + width], MULT)

        def quantize(rounded, width, name):
            codes = keep.tile([P, width], U32, name="codes" + name, tag="codes" + name, align_bytes=64)
            scales = keep.tile([P, width], U8, name="scales" + name, align_bytes=64)
            nc.vector.quantize_mx(out=codes[:].bitcast(FP8X4), scales=scales[:], in_=rounded.rearrange("p j i -> p (j i)"))
            return codes, scales

        def project(operand, at):
            codes, scales = operand
            bank = psum.tile([P, PACK, PIECE], F32, name="bank", tag="bank")
            for t in range(PACK):
                nc.tensor.matmul_mx(
                    out=bank[:, t, :],
                    lhsT=w_codes[:, 2 * P * t : 2 * P * (t + 1)].bitcast(FP4X4),
                    lhsT_scale=w_plane[:, P * t : P * (t + 1)],
                    rhs=codes[:, at : at + PIECE].bitcast(FP8X4),
                    rhs_scale=scales[:, at : at + PIECE],
                    start=True,
                    stop=True,
                )
            return bank

        EARLY = 2 * J + PIECE
        LATE = J - PIECE
        flat = keep.tile([P, HALF + PACK * EARLY], F32, name="flat")
        picked = flat[:, HALF:].rearrange("p (i j) -> p i j", i=PACK)
        late = flat[:, 0 : PACK * LATE].rearrange("p (i j) -> p i j", i=PACK)
        operands = {}
        first = {}
        of_two = {}
        of_three = {}

        rounded = [keep.tile([P, J + PIECE, PACK], BF16, name="rounded%d" % c, align_bytes=64) for c in range(PICKS)]

        def round_rows(c, j0, src):
            width = src.shape[2]
            nc.scalar.copy(
                out=rounded[c][:, j0 : j0 + width, :].rearrange("p (a e) i -> p a i e", e=2),
                in_=src.rearrange("p i (a e) -> p a i e", e=2),
            )

        def hold_first(k):
            bank = project(operands[0, k // 2], (k % 2) * PIECE)
            first[k] = keep.tile([P, PACK, PIECE], F32, name="first%d" % k)
            nc.scalar.copy(out=first[k][:], in_=bank[:])

        def freed(at):
            return flat[:, at : at + J].rearrange("p (t j) -> p t j", t=PACK)

        seconds = {}

        def part_of_two(k, t0, t1):
            nc.vector.tensor_tensor(of_two[k][:, t0:t1, :], seconds[k][:, t0:t1, :], first[k][:, t0:t1, :], MAX)

        def max_of_two(k):
            second = project(operands[1], k * PIECE)
            if k >= 2:
                of_two[k] = freed((k - 1) * J)
            else:
                of_two[k] = keep.tile([P, PACK, PIECE], F32, name="of_two%d" % k)[:]
            seconds[k] = second
            part_of_two(k, 0, 2 if k == 3 else PACK)

        def max_of_three(k):
            third = project(operands[2, min(k, 2)], PIECE if k == 3 else 0)
            if k == 1:
                of_three[k] = freed(0)
            else:
                of_three[k] = keep.tile([P, PACK, PIECE], F32, name="of_three%d" % k)[:]
            step = (PACK, 2, 2, 1)[k]
            for t0 in range(0, PACK, step):
                t1 = t0 + step
                nc.vector.tensor_tensor(of_three[k][:, t0:t1, :], third[:, t0:t1, :], of_two[k][:, t0:t1, :], MAX)

        y_plane = keep.tile([P, J], U8, name="y_plane", align_bytes=64)
        out_rows = out_0.rearrange("(p t) j -> p t j", t=PACK)
        out_words = out_1[0].rearrange("p j i -> p (j i)").bitcast(I32)

        y_rounded = [rounded[2][:, J - PIECE :, :], keep.tile([P, HALF, PACK], BF16, name="y_rounded1", align_bytes=64)[:]]

        def finish(k):
            j0 = k * PIECE
            y = keep.tile([P, PACK, PIECE], F32, name="y%d" % k)
            for t in range(PACK):
                nc.scalar.activation(out=y[:, t, :], in_=of_three[k][:, t, :], func=GELU, bias=bias[:, t : t + 1])
            for t0, t1 in ((0, 2), (2, 4)) if k == 1 else ((0, 4),):
                nc.sync.dma_start(out=out_rows[:, t0:t1, j0 : j0 + PIECE], in_=y[:, t0:t1, :])
            return y

        def round_on_pool(dst, src):
            nc.gpsimd.tensor_scalar(dst, src.rearrange("p i j -> p j i"), 1.0, 0.0, MULT, ADD)

        def round_y(copy, y, k, lo, hi):
            at = (k % 2) * PIECE
            copy(
                out=y_rounded[k // 2][:, at + lo : at + hi, :].rearrange("p (a e) t -> p a t e", e=4),
                in_=y[:, :, lo:hi].rearrange("p t (a e) -> p a t e", e=4),
            )

        y_codes = [keep.tile([P, HALF], U32, name="y_codes%d" % h, align_bytes=64) for h in range(2)]

        def hand_on(j0, width):
            at = j0 % HALF
            nc.vector.quantize_mx(
                out=y_codes[j0 // HALF][:, at : at + width].bitcast(FP8X4),
                scales=y_plane[:, j0 : j0 + width],
                in_=y_rounded[j0 // HALF][:, at : at + width, :].rearrange("p j t -> p (j t)"),
            )
            if at + width == HALF:
                nc.sync.dma_start(out=out_words[:, j0 - at : j0 - at + HALF], in_=y_codes[j0 // HALF][:].bitcast(I32))

        for j0, j1 in ((0, J), (J, 2 * J), (2 * J, EARLY)):
            gather(picked[:, 0, j0:j1], 0, 0, j0, j1 - j0)
        for i in (1, 2):
            gather(picked[:, i, :], i, 0, 0, EARLY)
        for j0, j1 in ((0, PIECE), (PIECE, J), (J, EARLY)):
            gather(picked[:, 3, j0:j1], 3, 0, j0, j1 - j0)
        for j0, j1 in ((0, PIECE), (PIECE, HALF), (HALF, J)):
            round_rows(0, j0, picked[:, :, j0:j1])
        for h in range(2):
            operands[0, h] = quantize(rounded[0][:, h * HALF : (h + 1) * HALF, :], HALF, "0_%d" % h)
        for j0, j1 in ((0, LATE), (LATE, J)):
            round_rows(1, j0, picked[:, :, J + j0 : J + j1])
        operands[1] = quantize(rounded[1][:, 0:J, :], J, "1")
        round_rows(2, 0, picked[:, :, 2 * J :])
        operands[2, 0] = quantize(rounded[2][:, 0:PIECE, :], PIECE, "2_0")
        for i in range(PACK):
            gather(late[:, i, :], i, 2, PIECE, LATE)
        for k in range(3):
            hold_first(k)
        for k in (0, 1):
            max_of_two(k)
        max_of_three(0)
        round_rows(2, PIECE, late[:, :, 0 : LATE // 2])
        round_on_pool(rounded[2][:, J - LATE // 2 : J, :], late[:, :, LATE // 2 :])
        hold_first(3)
        operands[2, 1] = quantize(rounded[2][:, PIECE:HALF, :], PIECE, "2_1")
        operands[2, 2] = quantize(rounded[2][:, HALF:J, :], HALF, "2_2")
        max_of_two(2)
        max_of_three(1)
        max_of_three(2)
        max_of_two(3)
        part_of_two(3, 2, PACK)
        max_of_three(3)
        ys = {k: finish(k) for k in (0, 1)}
        for k in (0, 1):
            round_on_pool(y_rounded[0][:, k * PIECE : (k + 1) * PIECE, :], ys[k][:])
        for k in (2, 3):
            ys[k] = finish(k)
        round_y(nc.vector.tensor_copy, ys[2], 2, 0, PIECE)
        hand_on(0, HALF)
        round_y(nc.scalar.copy, ys[3], 3, 0, PIECE // 2)
        round_y(nc.vector.tensor_copy, ys[3], 3, PIECE // 2, PIECE)
        hand_on(HALF, PIECE)
        hand_on(HALF + PIECE, PIECE)
        for q in range(4):
            queue = nc.scalar if q % 2 else nc.sync
            queue.dma_start(out=out_2[0, 4 * q : 4 * q + 4, :].bitcast(I32), in_=y_plane[32 * q : 32 * q + 4, :].bitcast(I32))
